import numpy as np
import ml_dtypes


def mxq(x, axis, fmt="e4m3"):
    dtype, down = {"e4m3": (ml_dtypes.float8_e4m3fn, 7), "e5m2": (ml_dtypes.float8_e5m2, 14)}[fmt]
    v = np.moveaxis(np.asarray(x, np.float32).astype(ml_dtypes.bfloat16).astype(np.float64), axis, -1)
    blocks = v.reshape(v.shape[:-1] + (-1, 32))
    amax = np.abs(blocks).max(-1, keepdims=True)
    byte = np.maximum(np.where(amax > 0, np.frexp(amax)[1] - 1 + 127, 0) - down, 1)
    scale = np.exp2(byte - 127.0)
    codes = (blocks / scale).astype(np.float32).astype(dtype).astype(np.float64)
    return np.moveaxis((codes * scale).reshape(v.shape), -1, axis)


WIDE = False


def mx_kscale(k):
    if not WIDE:
        return np.ones(k)
    levels = np.array([10, -10, 5, -5, 0])
    if k % 512:
        return np.exp2(np.random.permutation(np.resize(levels, k // 32))).repeat(32)
    a = np.empty((k // 512, 16))
    for p in range(k // 512):
        a[p, :8] = np.random.permutation(np.resize(levels, 8))
        for g in range(8):
            far = levels[np.abs(levels - a[p, g]) >= 10]
            a[p, g + 8] = far[np.random.randint(len(far))]
    return np.exp2(a.ravel()).repeat(32)


def f64(x):
    return np.asarray(x).astype(np.float64)


def striped(idx):
    return np.tile(idx.reshape(-1, 16).T, (8, 1)).astype(np.uint16)


def unstriped(offs):
    return offs[:16].T.reshape(-1).astype(np.int64)


E2M1 = np.array([0.0, 0.5, 1.0, 1.5, 2.0, 3.0, 4.0, 6.0, -0.0, -0.5, -1.0, -1.5, -2.0, -3.0, -4.0, -6.0])


def pack_weight(w, fmt):
    k, n = w.shape
    w = f64(np.asarray(w, np.float32).astype(ml_dtypes.bfloat16)).reshape(k // 32, 32, n)
    amax = np.abs(w).max(1)
    if fmt == "e4m3":
        byte = np.frexp(amax)[1] - 1 + 127 - 7
    else:
        mant, ex = np.frexp(amax / 6.0)
        byte = np.where(mant > 0.5, ex, ex - 1) + 127
    byte = np.clip(np.where(amax > 0, byte, 1), 1, 254)
    scaled = (w * np.exp2(127.0 - byte)[:, None, :]).reshape(k, n).astype(np.float32)
    by_word = np.ascontiguousarray(scaled.reshape(k // 512, 128, 4, n).transpose(0, 1, 3, 2))
    if fmt == "e4m3":
        words = by_word.astype(ml_dtypes.float8_e4m3fn).view(np.uint8)
    else:
        c = by_word.astype(ml_dtypes.float4_e2m1fn).view(np.uint8) & 0xF
        words = (c[..., 0::2] | (c[..., 1::2] << 4)).reshape(k // 512, 128, 2 * n)
    return np.ascontiguousarray(words), np.ascontiguousarray(byte.astype(np.uint8).reshape(k // 512, 16, n))


def unpack_weight(words, scales, fmt):
    g, _, n = scales.shape
    words = np.ascontiguousarray(words).reshape(g, 128, n, -1)
    if fmt == "e4m3":
        vals = words.view(ml_dtypes.float8_e4m3fn).astype(np.float64)
    else:
        nib = np.empty((g, 128, n, 4), np.uint8)
        nib[..., 0::2] = words & 0xF
        nib[..., 1::2] = words >> 4
        vals = E2M1[nib]
    vals = vals * np.repeat(np.exp2(scales.astype(np.float64) - 127.0), 8, axis=1)[..., None]
    return vals.transpose(0, 1, 3, 2).reshape(g * 512, n)


def relu(v):
    return np.maximum(v, 0.0)


K, T, S, H, N = 512, 2048, 1024, 512, 512


def setup_inputs():
    n = np.random.standard_normal
    s = mx_kscale(K)
    u = mx_kscale(H)
    hard = np.random.permutation(T)[:S]
    x = pack_weight(n((K, T)) * s[:, None], "e4m3")
    w = pack_weight(n((K, N)) / np.sqrt(K) / s[:, None], "e2m1")
    return {
        "x_words": x[0],
        "x_scales": x[1],
        "w_words": w[0],
        "w_scales": w[1],
        "w1": (n((K, H)) / np.sqrt(K) / s[:, None] * u).astype(np.float32),
        "w2": (n((H, N)) / np.sqrt(H) / u[:, None]).astype(np.float32),
        "offs": striped(hard),
    }


def reference(x_words, x_scales, w_words, w_scales, w1, w2, offs):
    w = unpack_weight(w_words, w_scales, "e2m1")
    w1q = mxq(f64(w1), 0, "e4m3")
    w2q = mxq(f64(w2), 0, "e4m3")
    idx = unstriped(offs)
    x = unpack_weight(x_words, x_scales, "e4m3")
    out = w.T @ x
    h = relu(w1q.T @ x[:, idx])
    out[:, idx] = w2q.T @ mxq(h, 0, "e4m3")
    return out

@@ -1,0 +1,201 @@
+from contextlib import ExitStack
+
+import concourse.mybir as mybir
+
+K, T, S, H, N = 512, 2048, 1024, 512, 512
+FLOPS = 2 * K * N * T + 2 * K * H * S + 2 * H * N * S
+
+F32 = mybir.dt.float32
+BF16 = mybir.dt.bfloat16
+I32 = mybir.dt.int32
+U32 = mybir.dt.uint32
+U16 = mybir.dt.uint16
+U8 = mybir.dt.uint8
+FP8X4 = mybir.dt.float8_e4m3fn_x4
+FP4X4 = mybir.dt.float4_e2m1fn_x4
+COPY = mybir.ActivationFunctionType.Copy
+RELU = mybir.ActivationFunctionType.Relu
+
+P = 128
+PACK = 4
+BANK = 512
+CHUNK = 256
+STRIPE = 16
+
+
+def tile_moe_cas_mlp_relu_kernel(
+    tc, x_words, x_scales, w_words, w_scales, w1, w2, offs, out
+):
+    nc = tc.nc
+    with ExitStack() as ctx:
+        keep = ctx.enter_context(tc.tile_pool(name="keep", bufs=1))
+        shared = ctx.enter_context(tc.tile_pool(name="shared", bufs=1))
+        psum = ctx.enter_context(tc.psum_pool(name="psum", bufs=1))
+
+        def held(name, shape, dtype):
+            return keep.tile(shape, dtype, name=name, align_bytes=64)
+
+        def placed(name, shape, dtype, offset):
+            return shared.tile(shape, dtype, name=name, align_bytes=64, offset=offset)
+
+        offsets = keep.tile([P, S // STRIPE], U16)
+        x_codes = held("x_codes", [P, T], I32)
+        x_plane = held("x_plane", [P, T], U8)
+        w_codes = held("w_codes", [P, 2 * N], U8)
+        w_plane = held("w_plane", [P, N], U8)
+        w1_raw = held("w1_raw", [P, PACK, H], F32)
+        w2_raw = held("w2_raw", [P, PACK, N], F32)
+        w1_codes = held("w1_codes", [P, H], U32)
+        w1_plane = held("w1_plane", [P, H], U8)
+        w2_codes = held("w2_codes", [P, N], U32)
+        w2_plane = held("w2_plane", [P, N], U8)
+        h_codes = held("h_codes", [P, S], U32)
+        h_plane = held("h_plane", [P, S], U8)
+        z_rows = [held("z_rows%d" % t, [P, S], F32) for t in range(N // P)]
+        result = [held("result%d" % t, [P, T], F32) for t in range(N // P)]
+        banks = [psum.tile([P, BANK], F32, name="bank%d" % b) for b in range(8)]
+        used = []
+
+        def next_bank():
+            used.append(len(used))
+            return banks[used[-1] % len(banks)]
+
+        nc.vector.memset(x_plane[:].bitcast(I32), 0)
+        nc.gpsimd.memset(w_plane[:].bitcast(I32), 0)
+        nc.sync.dma_start(offsets[:], offs)
+        nc.sync.dma_start(w_codes[:].bitcast(I32), w_words[0].bitcast(I32))
+        nc.sync.dma_start(x_codes[:], x_words[0].rearrange("p t d -> p (t d)").bitcast(I32))
+        for r in range(PACK):
+            nc.scalar.dma_start(
+                x_plane[r:P:32, :].bitcast(I32), x_scales[0, r:16:PACK, :].bitcast(I32)
+            )
+        for r in range(PACK):
+            nc.gpsimd.dma_start(
+                w_plane[r:P:32, :].bitcast(I32), w_scales[0, r:16:PACK, :].bitcast(I32)
+            )
+        nc.sync.dma_start(w1_raw[:], w1.rearrange("(p j) c -> p j c", j=PACK))
+        nc.sync.dma_start(w2_raw[:], w2.rearrange("(p j) c -> p j c", j=PACK))
+
+        W1_AT, H_AT, STAGE = 0, 4096, 2048
+        gathered = {}
+
+        def listed(first, count):
+            return offsets[:, first // STRIPE : (first + count) // STRIPE]
+
+        def gather(c, offset=None):
+            if offset is None:
+                codes = held("g_codes%d" % c, [P, CHUNK], U32)
+                plane = held("g_plane%d" % c, [P, CHUNK], U8)
+            else:
+                codes = placed("g_codes%d" % c, [P, CHUNK], U32, offset)
+                plane = placed("g_plane%d" % c, [P, CHUNK], U8, offset + 4 * CHUNK)
+            gathered[c] = (codes, plane)
+            nc.vector.tensor_copy(codes[:], x_codes[:].bitcast(U32).indirect(listed(c * CHUNK, CHUNK)))
+            nc.vector.tensor_copy(plane[:], x_plane[:].indirect(listed(c * CHUNK, CHUNK)))
+
+        def prepare_w1():
+            w1_bf = placed("w1_bf", [P, H * PACK], BF16, W1_AT)
+            dst = w1_bf[:].rearrange("p (t m j) -> p m j t", t=PACK, j=PACK)
+            src = w1_raw[:].rearrange("p j (m t) -> p m j t", t=PACK)
+            nc.vector.tensor_copy(dst, src)
+            nc.vector.quantize_mx(out=w1_codes[:].bitcast(FP8X4), scales=w1_plane[:], in_=w1_bf[:])
+
+        def prepare_w2(first, count, copy, offset):
+            cols = slice(first, first + count)
+            w2_bf = placed("w2_bf%d" % first, [P, count * PACK], BF16, offset)
+            dst = w2_bf[:].rearrange("p (c i j) -> p c j i", i=4, j=PACK)
+            src = w2_raw[:, :, cols].rearrange("p j (c i) -> p c j i", i=4)
+            copy(dst, src)
+            nc.vector.quantize_mx(
+                out=w2_codes[:, cols].bitcast(FP8X4), scales=w2_plane[:, cols], in_=w2_bf[:]
+            )
+
+        def light(t, start, stop):
+            for first in range(start, stop, BANK):
+                tokens = slice(first, first + BANK)
+                y_acc = next_bank()
+                nc.tensor.matmul_mx(
+                    out=y_acc[:],
+                    lhsT=w_codes[:, 2 * t * P : 2 * (t + 1) * P].bitcast(FP4X4),
+                    lhsT_scale=w_plane[:, t * P : (t + 1) * P],
+                    rhs=x_codes[:, tokens].bitcast(FP8X4),
+                    rhs_scale=x_plane[:, tokens],
+                    start=True,
+                    stop=True,
+                )
+                nc.scalar.activation(result[t][:, tokens], y_acc[:], COPY)
+
+        def hidden(c):
+            codes, plane = gathered[c]
+            h_bf = placed("h_bf%d" % c, [P, CHUNK * PACK], BF16, H_AT + c * STAGE)
+            for base in range(0, CHUNK, P):
+                h_acc = next_bank()
+                for j in range(PACK):
+                    nc.tensor.matmul_mx(
+                        out=h_acc[:, j * P : (j + 1) * P],
+                        lhsT=w1_codes[:, j * P : (j + 1) * P].bitcast(FP8X4),
+                        lhsT_scale=w1_plane[:, j * P : (j + 1) * P],
+                        rhs=codes[:, base : base + P].bitcast(FP8X4),
+                        rhs_scale=plane[:, base : base + P],
+                        start=True,
+                        stop=True,
+                    )
+                dst = h_bf[:, base * PACK : (base + P) * PACK].rearrange("p (s j) -> p s j", j=PACK)
+                nc.scalar.activation(dst, h_acc[:].rearrange("p (j s) -> p s j", j=PACK), RELU)
+            slots = slice(c * CHUNK, (c + 1) * CHUNK)
+            nc.vector.quantize_mx(
+                out=h_codes[:, slots].bitcast(FP8X4), scales=h_plane[:, slots], in_=h_bf[:]
+            )
+
+        def heavy(t, first, count):
+            slots = slice(first, first + count)
+            z_acc = next_bank()
+            nc.tensor.matmul_mx(
+                out=z_acc[:, :count],
+                lhsT=w2_codes[:, t * P : (t + 1) * P].bitcast(FP8X4),
+                lhsT_scale=w2_plane[:, t * P : (t + 1) * P],
+                rhs=h_codes[:, slots].bitcast(FP8X4),
+                rhs_scale=h_plane[:, slots],
+                start=True,
+                stop=True,
+            )
+            nc.scalar.copy(z_rows[t][:, slots], z_acc[:, :count])
+
+        def scatter(t, first, count):
+            nc.vector.tensor_copy(
+                result[t][:].indirect(listed(first, count)), z_rows[t][:, first : first + count]
+            )
+
+        def store(t):
+            nc.sync.dma_start(out[t * P : (t + 1) * P, :], result[t][:])
+
+        gather(0)
+        gather(1)
+        prepare_w1()
+        gather(2, W1_AT)
+        light(0, 0, T)
+        prepare_w2(0, P, nc.vector.tensor_copy, H_AT + 4 * STAGE)
+        hidden(0)
+        gather(3, H_AT)
+        for c in range(S // CHUNK):
+            if c + 1 < S // CHUNK:
+                hidden(c + 1)
+            else:
+                prepare_w2(P, P, nc.scalar.copy, H_AT + STAGE)
+                light(1, 0, T // 2)
+            heavy(0, c * CHUNK, CHUNK)
+            scatter(0, c * CHUNK, CHUNK)
+        store(0)
+        light(1, T // 2, T)
+        heavy(1, 0, BANK)
+        scatter(1, 0, BANK)
+        prepare_w2(2 * P, 2 * P, nc.scalar.copy, H_AT + 2 * STAGE)
+        heavy(1, BANK, BANK)
+        scatter(1, BANK, BANK)
+        store(1)
+        for t in range(2, N // P):
+            light(t, 0, T)
+            for first in range(0, S, BANK):
+                heavy(t, first, BANK)
+            scatter(t, 0, S)
+            store(t)

@@ -21,6 +21,7 @@ PACK = 4
 BANK = 512
 CHUNK = 256
 STRIPE = 16
+SPLIT = 84
 
 
 def tile_moe_cas_mlp_relu_kernel(
@@ -38,13 +39,13 @@ def tile_moe_cas_mlp_relu_kernel(
         def placed(name, shape, dtype, offset):
             return shared.tile(shape, dtype, name=name, align_bytes=64, offset=offset)
 
+        W1_AT, H_AT, STAGE, RAW_AT = 0, 4096, 2048, 16384
         offsets = keep.tile([P, S // STRIPE], U16)
         x_codes = held("x_codes", [P, T], I32)
         x_plane = held("x_plane", [P, T], U8)
         w_codes = held("w_codes", [P, 2 * N], U8)
         w_plane = held("w_plane", [P, N], U8)
-        w1_raw = held("w1_raw", [P, PACK, H], F32)
-        w2_raw = held("w2_raw", [P, PACK, N], F32)
+        w1_raw = placed("w1_raw", [P, PACK, H], F32, RAW_AT)
         w1_codes = held("w1_codes", [P, H], U32)
         w1_plane = held("w1_plane", [P, H], U8)
         w2_codes = held("w2_codes", [P, N], U32)
@@ -58,25 +59,23 @@ def tile_moe_cas_mlp_relu_kernel(
 
         def next_bank():
             used.append(len(used))
-            return banks[used[-1] % len(banks)]
+            return banks[(used[-1] - (2 if used[-1] >= 4 else 0)) % len(banks) if used[-1] != 5 else 7]
 
         nc.vector.memset(x_plane[:].bitcast(I32), 0)
         nc.gpsimd.memset(w_plane[:].bitcast(I32), 0)
+        nc.sync.dma_start(w1_raw[:], w1.rearrange("(p j) c -> p j c", j=PACK))
         nc.sync.dma_start(offsets[:], offs)
         nc.sync.dma_start(w_codes[:].bitcast(I32), w_words[0].bitcast(I32))
-        nc.sync.dma_start(x_codes[:], x_words[0].rearrange("p t d -> p (t d)").bitcast(I32))
         for r in range(PACK):
-            nc.scalar.dma_start(
-                x_plane[r:P:32, :].bitcast(I32), x_scales[0, r:16:PACK, :].bitcast(I32)
-            )
-        for r in range(PACK):
-            nc.gpsimd.dma_start(
+            nc.sync.dma_start(
                 w_plane[r:P:32, :].bitcast(I32), w_scales[0, r:16:PACK, :].bitcast(I32)
             )
-        nc.sync.dma_start(w1_raw[:], w1.rearrange("(p j) c -> p j c", j=PACK))
-        nc.sync.dma_start(w2_raw[:], w2.rearrange("(p j) c -> p j c", j=PACK))
+        nc.sync.dma_start(x_codes[:], x_words[0].rearrange("p t d -> p (t d)").bitcast(I32))
+        for r in range(PACK):
+            nc.sync.dma_start(
+                x_plane[r:P:32, :].bitcast(I32), x_scales[0, r:16:PACK, :].bitcast(I32)
+            )
 
-        W1_AT, H_AT, STAGE = 0, 4096, 2048
         gathered = {}
 
         def listed(first, count):
@@ -97,7 +96,8 @@ def tile_moe_cas_mlp_relu_kernel(
             w1_bf = placed("w1_bf", [P, H * PACK], BF16, W1_AT)
             dst = w1_bf[:].rearrange("p (t m j) -> p m j t", t=PACK, j=PACK)
             src = w1_raw[:].rearrange("p j (m t) -> p m j t", t=PACK)
-            nc.vector.tensor_copy(dst, src)
+            nc.vector.tensor_copy(dst[:, :SPLIT], src[:, :SPLIT])
+            nc.scalar.activation(dst[:, SPLIT:], src[:, SPLIT:], COPY)
             nc.vector.quantize_mx(out=w1_codes[:].bitcast(FP8X4), scales=w1_plane[:], in_=w1_bf[:])
 
         def prepare_w2(first, count, copy, offset):
@@ -169,10 +169,12 @@ def tile_moe_cas_mlp_relu_kernel(
         def store(t):
             nc.sync.dma_start(out[t * P : (t + 1) * P, :], result[t][:])
 
+        prepare_w1()
+        w2_raw = placed("w2_raw", [P, PACK, N], F32, RAW_AT)
+        nc.sync.dma_start(w2_raw[:], w2.rearrange("(p j) c -> p j c", j=PACK))
         gather(0)
         gather(1)
-        prepare_w1()
-        gather(2, W1_AT)
+        gather(2)
         light(0, 0, T)
         prepare_w2(0, P, nc.vector.tensor_copy, H_AT + 4 * STAGE)
         hidden(0)

@@ -39,13 +39,13 @@ def tile_moe_cas_mlp_relu_kernel(
         def placed(name, shape, dtype, offset):
             return shared.tile(shape, dtype, name=name, align_bytes=64, offset=offset)
 
-        W1_AT, H_AT, STAGE, RAW_AT = 0, 4096, 2048, 16384
+        W1_AT, H_AT, STAGE, RAW_AT = 0, 8192, 2048, 0
         offsets = keep.tile([P, S // STRIPE], U16)
         x_codes = held("x_codes", [P, T], I32)
         x_plane = held("x_plane", [P, T], U8)
         w_codes = held("w_codes", [P, 2 * N], U8)
         w_plane = held("w_plane", [P, N], U8)
-        w1_raw = placed("w1_raw", [P, PACK, H], F32, RAW_AT)
+        w1_raw = held("w1_raw", [P, PACK, H], F32)
         w1_codes = held("w1_codes", [P, H], U32)
         w1_plane = held("w1_plane", [P, H], U8)
         w2_codes = held("w2_codes", [P, N], U32)
@@ -81,16 +81,11 @@ def tile_moe_cas_mlp_relu_kernel(
         def listed(first, count):
             return offsets[:, first // STRIPE : (first + count) // STRIPE]
 
-        def gather(c, offset=None):
-            if offset is None:
-                codes = held("g_codes%d" % c, [P, CHUNK], U32)
-                plane = held("g_plane%d" % c, [P, CHUNK], U8)
-            else:
-                codes = placed("g_codes%d" % c, [P, CHUNK], U32, offset)
-                plane = placed("g_plane%d" % c, [P, CHUNK], U8, offset + 4 * CHUNK)
-            gathered[c] = (codes, plane)
-            nc.vector.tensor_copy(codes[:], x_codes[:].bitcast(U32).indirect(listed(c * CHUNK, CHUNK)))
-            nc.vector.tensor_copy(plane[:], x_plane[:].indirect(listed(c * CHUNK, CHUNK)))
+        def gather_words(codes, first, count):
+            nc.vector.tensor_copy(codes, x_codes[:].bitcast(U32).indirect(listed(first, count)))
+
+        def gather_scales(plane, first, count):
+            nc.vector.tensor_copy(plane, x_plane[:].indirect(listed(first, count)))
 
         def prepare_w1():
             w1_bf = placed("w1_bf", [P, H * PACK], BF16, W1_AT)
@@ -171,14 +166,26 @@ def tile_moe_cas_mlp_relu_kernel(
 
         prepare_w1()
         w2_raw = placed("w2_raw", [P, PACK, N], F32, RAW_AT)
-        nc.sync.dma_start(w2_raw[:], w2.rearrange("(p j) c -> p j c", j=PACK))
-        gather(0)
-        gather(1)
-        gather(2)
+        w2_rows = w2.rearrange("(p j) c -> p j c", j=PACK)
+        nc.sync.dma_start(w2_raw[:, :, :P], w2_rows[:, :, :P])
+        nc.sync.dma_start(w2_raw[:, :, P:], w2_rows[:, :, P:])
+        early = S - CHUNK
+        early_codes = held("early_codes", [P, early], U32)
+        early_plane = held("early_plane", [P, early], U8)
+        gather_words(early_codes[:], 0, early)
+        gather_scales(early_plane[:, :CHUNK], 0, CHUNK)
+        gather_scales(early_plane[:, CHUNK:], CHUNK, early - CHUNK)
+        for c in range(early // CHUNK):
+            slots = slice(c * CHUNK, (c + 1) * CHUNK)
+            gathered[c] = (early_codes[:, slots], early_plane[:, slots])
         light(0, 0, T)
         prepare_w2(0, P, nc.vector.tensor_copy, H_AT + 4 * STAGE)
         hidden(0)
-        gather(3, H_AT)
+        late_codes = placed("late_codes", [P, CHUNK], U32, H_AT)
+        late_plane = placed("late_plane", [P, CHUNK], U8, H_AT + 4 * CHUNK)
+        gather_words(late_codes[:], early, CHUNK)
+        gather_scales(late_plane[:], early, CHUNK)
+        gathered[early // CHUNK] = (late_codes[:], late_plane[:])
         for c in range(S // CHUNK):
             if c + 1 < S // CHUNK:
                 hidden(c + 1)
@@ -191,7 +198,7 @@ def tile_moe_cas_mlp_relu_kernel(
         light(1, T // 2, T)
         heavy(1, 0, BANK)
         scatter(1, 0, BANK)
-        prepare_w2(2 * P, 2 * P, nc.scalar.copy, H_AT + 2 * STAGE)
+        prepare_w2(2 * P, 2 * P, nc.scalar.copy, H_AT + STAGE)
         heavy(1, BANK, BANK)
         scatter(1, BANK, BANK)
         store(1)

@@ -59,7 +59,7 @@ def tile_moe_cas_mlp_relu_kernel(
 
         def next_bank():
             used.append(len(used))
-            return banks[(used[-1] - (2 if used[-1] >= 4 else 0)) % len(banks) if used[-1] != 5 else 7]
+            return banks[used[-1] % len(banks)]
 
         nc.vector.memset(x_plane[:].bitcast(I32), 0)
         nc.gpsimd.memset(w_plane[:].bitcast(I32), 0)

@@ -21,7 +21,8 @@ PACK = 4
 BANK = 512
 CHUNK = 256
 STRIPE = 16
-SPLIT = 84
+SPLIT = 24
+ROTATION = (7, 2, 3, 4, 5, 0, 1, 6)
 
 
 def tile_moe_cas_mlp_relu_kernel(
@@ -39,44 +40,56 @@ def tile_moe_cas_mlp_relu_kernel(
         def placed(name, shape, dtype, offset):
             return shared.tile(shape, dtype, name=name, align_bytes=64, offset=offset)
 
-        W1_AT, H_AT, STAGE, RAW_AT = 0, 8192, 2048, 0
+        W1_AT, H_AT, STAGE, RAW_AT = 0, 8192, 2048, 16384
         offsets = keep.tile([P, S // STRIPE], U16)
         x_codes = held("x_codes", [P, T], I32)
         x_plane = held("x_plane", [P, T], U8)
         w_codes = held("w_codes", [P, 2 * N], U8)
         w_plane = held("w_plane", [P, N], U8)
-        w1_raw = held("w1_raw", [P, PACK, H], F32)
+        w1_raw = [
+            held("w1_raw0", [P, PACK, H // 2], F32),
+            placed("w1_raw1", [P, PACK, H // 2], F32, RAW_AT),
+        ]
+        w2_head = held("w2_head", [P, PACK, P], F32)
+        w2_rest = held("w2_rest", [P, PACK, N - P], F32)
         w1_codes = held("w1_codes", [P, H], U32)
         w1_plane = held("w1_plane", [P, H], U8)
-        w2_codes = held("w2_codes", [P, N], U32)
         w2_plane = held("w2_plane", [P, N], U8)
         h_codes = held("h_codes", [P, S], U32)
         h_plane = held("h_plane", [P, S], U8)
         z_rows = [held("z_rows%d" % t, [P, S], F32) for t in range(N // P)]
-        result = [held("result%d" % t, [P, T], F32) for t in range(N // P)]
+        result = [placed("result%d" % t, [P, T], F32, RAW_AT + t * T * 4) for t in range(N // P)]
         banks = [psum.tile([P, BANK], F32, name="bank%d" % b) for b in range(8)]
         used = []
 
-        def next_bank():
-            used.append(len(used))
-            return banks[used[-1] % len(banks)]
+        def turn(count):
+            first = len(used)
+            used.extend(range(count))
+            return [ROTATION[(first + b) % len(ROTATION)] for b in range(count)]
 
         nc.vector.memset(x_plane[:].bitcast(I32), 0)
         nc.gpsimd.memset(w_plane[:].bitcast(I32), 0)
-        nc.sync.dma_start(w1_raw[:], w1.rearrange("(p j) c -> p j c", j=PACK))
+        w1_rows = w1.rearrange("(p j) c -> p j c", j=PACK)
+        w2_rows = w2.rearrange("(p j) c -> p j c", j=PACK)
         nc.sync.dma_start(offsets[:], offs)
-        nc.sync.dma_start(w_codes[:].bitcast(I32), w_words[0].bitcast(I32))
-        for r in range(PACK):
-            nc.sync.dma_start(
-                w_plane[r:P:32, :].bitcast(I32), w_scales[0, r:16:PACK, :].bitcast(I32)
-            )
-        nc.sync.dma_start(x_codes[:], x_words[0].rearrange("p t d -> p (t d)").bitcast(I32))
+        for half in (slice(0, N // 4), slice(N // 4, N // 2)):
+            nc.sync.dma_start(w_codes[:].bitcast(I32)[:, half], w_words[0].bitcast(I32)[:, half])
         for r in range(PACK):
             nc.sync.dma_start(
                 x_plane[r:P:32, :].bitcast(I32), x_scales[0, r:16:PACK, :].bitcast(I32)
             )
+        nc.sync.dma_start(x_codes[:], x_words[0].rearrange("p t d -> p (t d)").bitcast(I32))
+        for r in range(PACK):
+            nc.sync.dma_start(
+                w_plane[r:P:32, :].bitcast(I32), w_scales[0, r:16:PACK, :].bitcast(I32)
+            )
+        for u in range(2):
+            nc.sync.dma_start(w1_raw[u][:], w1_rows[:, :, u * H // 2 : (u + 1) * H // 2])
+        nc.sync.dma_start(w2_head[:], w2_rows[:, :, :P])
+        nc.sync.dma_start(w2_rest[:], w2_rows[:, :, P:])
 
         gathered = {}
+        w2_codes = {}
 
         def listed(first, count):
             return offsets[:, first // STRIPE : (first + count) // STRIPE]
@@ -90,25 +103,37 @@ def tile_moe_cas_mlp_relu_kernel(
         def prepare_w1():
             w1_bf = placed("w1_bf", [P, H * PACK], BF16, W1_AT)
             dst = w1_bf[:].rearrange("p (t m j) -> p m j t", t=PACK, j=PACK)
-            src = w1_raw[:].rearrange("p j (m t) -> p m j t", t=PACK)
-            nc.vector.tensor_copy(dst[:, :SPLIT], src[:, :SPLIT])
-            nc.scalar.activation(dst[:, SPLIT:], src[:, SPLIT:], COPY)
-            nc.vector.quantize_mx(out=w1_codes[:].bitcast(FP8X4), scales=w1_plane[:], in_=w1_bf[:])
+            src = [raw[:].rearrange("p j (m t) -> p m j t", t=PACK) for raw in w1_raw]
+            half = P // 2
+            nc.scalar.activation(dst[:, :half], src[0], COPY)
+            nc.scalar.activation(dst[:, half : half + SPLIT], src[1][:, :SPLIT], COPY)
+            nc.vector.tensor_copy(dst[:, half + SPLIT :], src[1][:, SPLIT:])
+            for t in range(PACK):
+                cols = slice(t * P, (t + 1) * P)
+                nc.vector.quantize_mx(
+                    out=w1_codes[:, cols].bitcast(FP8X4),
+                    scales=w1_plane[:, cols],
+                    in_=w1_bf[:, t * H : (t + 1) * H],
+                )
 
-        def prepare_w2(first, count, copy, offset):
-            cols = slice(first, first + count)
+        def stage_w2(first, count, copy, offset):
+            raw = w2_head[:] if first == 0 else w2_rest[:, :, first - P : first - P + count]
             w2_bf = placed("w2_bf%d" % first, [P, count * PACK], BF16, offset)
             dst = w2_bf[:].rearrange("p (c i j) -> p c j i", i=4, j=PACK)
-            src = w2_raw[:, :, cols].rearrange("p j (c i) -> p c j i", i=4)
-            copy(dst, src)
-            nc.vector.quantize_mx(
-                out=w2_codes[:, cols].bitcast(FP8X4), scales=w2_plane[:, cols], in_=w2_bf[:]
-            )
+            copy(dst, raw.rearrange("p j (c i) -> p c j i", i=4))
+            return w2_bf
 
-        def light(t, start, stop):
-            for first in range(start, stop, BANK):
-                tokens = slice(first, first + BANK)
-                y_acc = next_bank()
+        def quantize_w2(first, count, w2_bf, codes):
+            nc.vector.quantize_mx(
+                out=codes[:].bitcast(FP8X4), scales=w2_plane[:, first : first + count], in_=w2_bf[:]
+            )
+            for t in range(count // P):
+                w2_codes[first // P + t] = codes[:, t * P : (t + 1) * P]
+
+        def light(t, start, into, copy=nc.scalar.copy):
+            for b, bank in enumerate(into):
+                tokens = slice(start + b * BANK, start + (b + 1) * BANK)
+                y_acc = banks[bank]
                 nc.tensor.matmul_mx(
                     out=y_acc[:],
                     lhsT=w_codes[:, 2 * t * P : 2 * (t + 1) * P].bitcast(FP4X4),
@@ -118,13 +143,13 @@ def tile_moe_cas_mlp_relu_kernel(
                     start=True,
                     stop=True,
                 )
-                nc.scalar.activation(result[t][:, tokens], y_acc[:], COPY)
+                copy(result[t][:, tokens], y_acc[:])
 
-        def hidden(c):
+        def hidden(c, into):
             codes, plane = gathered[c]
             h_bf = placed("h_bf%d" % c, [P, CHUNK * PACK], BF16, H_AT + c * STAGE)
             for base in range(0, CHUNK, P):
-                h_acc = next_bank()
+                h_acc = banks[into[base // P]]
                 for j in range(PACK):
                     nc.tensor.matmul_mx(
                         out=h_acc[:, j * P : (j + 1) * P],
@@ -142,12 +167,12 @@ def tile_moe_cas_mlp_relu_kernel(
                 out=h_codes[:, slots].bitcast(FP8X4), scales=h_plane[:, slots], in_=h_bf[:]
             )
 
-        def heavy(t, first, count):
+        def heavy(t, first, count, bank):
             slots = slice(first, first + count)
-            z_acc = next_bank()
+            z_acc = banks[bank]
             nc.tensor.matmul_mx(
                 out=z_acc[:, :count],
-                lhsT=w2_codes[:, t * P : (t + 1) * P].bitcast(FP8X4),
+                lhsT=w2_codes[t].bitcast(FP8X4),
                 lhsT_scale=w2_plane[:, t * P : (t + 1) * P],
                 rhs=h_codes[:, slots].bitcast(FP8X4),
                 rhs_scale=h_plane[:, slots],
@@ -164,47 +189,50 @@ def tile_moe_cas_mlp_relu_kernel(
         def store(t):
             nc.sync.dma_start(out[t * P : (t + 1) * P, :], result[t][:])
 
-        prepare_w1()
-        w2_raw = placed("w2_raw", [P, PACK, N], F32, RAW_AT)
-        w2_rows = w2.rearrange("(p j) c -> p j c", j=PACK)
-        nc.sync.dma_start(w2_raw[:, :, :P], w2_rows[:, :, :P])
-        nc.sync.dma_start(w2_raw[:, :, P:], w2_rows[:, :, P:])
         early = S - CHUNK
         early_codes = held("early_codes", [P, early], U32)
-        early_plane = held("early_plane", [P, early], U8)
+        slot_plane = held("slot_plane", [P, S], U8)
+        gather_scales(slot_plane[:], 0, S)
         gather_words(early_codes[:], 0, early)
-        gather_scales(early_plane[:, :CHUNK], 0, CHUNK)
-        gather_scales(early_plane[:, CHUNK:], CHUNK, early - CHUNK)
         for c in range(early // CHUNK):
             slots = slice(c * CHUNK, (c + 1) * CHUNK)
-            gathered[c] = (early_codes[:, slots], early_plane[:, slots])
-        light(0, 0, T)
-        prepare_w2(0, P, nc.vector.tensor_copy, H_AT + 4 * STAGE)
-        hidden(0)
-        late_codes = placed("late_codes", [P, CHUNK], U32, H_AT)
-        late_plane = placed("late_plane", [P, CHUNK], U8, H_AT + 4 * CHUNK)
-        gather_words(late_codes[:], early, CHUNK)
-        gather_scales(late_plane[:], early, CHUNK)
-        gathered[early // CHUNK] = (late_codes[:], late_plane[:])
-        for c in range(S // CHUNK):
-            if c + 1 < S // CHUNK:
-                hidden(c + 1)
-            else:
-                prepare_w2(P, P, nc.scalar.copy, H_AT + STAGE)
-                light(1, 0, T // 2)
-            heavy(0, c * CHUNK, CHUNK)
-            scatter(0, c * CHUNK, CHUNK)
+            gathered[c] = (early_codes[:, slots], slot_plane[:, slots])
+        prepare_w1()
+        light(0, 0, (0, 1))
+        hidden(0, (2, 3))
+        w2_bf = stage_w2(0, P, nc.vector.tensor_copy, W1_AT + 1024)
+        light(0, 2 * BANK, (0, 1), nc.vector.tensor_copy)
+        quantize_w2(0, P, w2_bf, held("w2_codes0", [P, P], U32))
+        last_codes = placed("last_codes", [P, CHUNK], U32, H_AT)
+        gather_words(last_codes[:], early, CHUNK)
+        gathered[3] = (last_codes[:], slot_plane[:, early:])
+        hidden(1, (4, 5))
+        heavy(0, 0, CHUNK, 6)
+        scatter(0, 0, CHUNK)
+        hidden(2, turn(2))
+        heavy(0, CHUNK, CHUNK, *turn(1))
+        scatter(0, CHUNK, CHUNK)
+        hidden(3, turn(2))
+        heavy(0, 2 * CHUNK, CHUNK, *turn(1))
+        scatter(0, 2 * CHUNK, CHUNK)
+        light(1, 0, turn(1))
+        w2_bf = stage_w2(P, P, nc.scalar.copy, H_AT + 3 * STAGE)
+        quantize_w2(P, P, w2_bf, held("w2_codes1", [P, P], U32))
+        heavy(0, 3 * CHUNK, CHUNK, *turn(1))
+        scatter(0, 3 * CHUNK, CHUNK)
         store(0)
-        light(1, T // 2, T)
-        heavy(1, 0, BANK)
-        scatter(1, 0, BANK)
-        prepare_w2(2 * P, 2 * P, nc.scalar.copy, H_AT + STAGE)
-        heavy(1, BANK, BANK)
-        scatter(1, BANK, BANK)
+        light(1, BANK, turn(3))
+        heavy(1, 0, CHUNK, *turn(1))
+        scatter(1, 0, CHUNK)
+        w2_bf = stage_w2(2 * P, 2 * P, nc.scalar.copy, H_AT + 3 * STAGE)
+        quantize_w2(2 * P, 2 * P, w2_bf, held("w2_codes2", [P, 2 * P], U32))
+        heavy(1, CHUNK, CHUNK, *turn(1))
+        heavy(1, BANK, BANK, *turn(1))
+        scatter(1, CHUNK, early)
         store(1)
         for t in range(2, N // P):
-            light(t, 0, T)
-            for first in range(0, S, BANK):
-                heavy(t, first, BANK)
+            light(t, 0, turn(4))
+            heavy(t, 0, BANK, *turn(1))
+            heavy(t, BANK, BANK, *turn(1))
             scatter(t, 0, S)
             store(t)

@@ -40,7 +40,7 @@ def tile_moe_cas_mlp_relu_kernel(
         def placed(name, shape, dtype, offset):
             return shared.tile(shape, dtype, name=name, align_bytes=64, offset=offset)
 
-        W1_AT, H_AT, STAGE, RAW_AT = 0, 8192, 2048, 16384
+        W1_AT, W2_AT, H_AT, STAGE, RAW_AT = 0, 4096, 8192, 2048, 16384
         offsets = keep.tile([P, S // STRIPE], U16)
         x_codes = held("x_codes", [P, T], I32)
         x_plane = held("x_plane", [P, T], U8)
@@ -72,8 +72,8 @@ def tile_moe_cas_mlp_relu_kernel(
         w1_rows = w1.rearrange("(p j) c -> p j c", j=PACK)
         w2_rows = w2.rearrange("(p j) c -> p j c", j=PACK)
         nc.sync.dma_start(offsets[:], offs)
-        for half in (slice(0, N // 4), slice(N // 4, N // 2)):
-            nc.sync.dma_start(w_codes[:].bitcast(I32)[:, half], w_words[0].bitcast(I32)[:, half])
+        nc.sync.dma_start(w_codes[:].bitcast(I32), w_words[0].bitcast(I32))
+        nc.sync.dma_start(w2_head[:], w2_rows[:, :, :P])
         for r in range(PACK):
             nc.sync.dma_start(
                 x_plane[r:P:32, :].bitcast(I32), x_scales[0, r:16:PACK, :].bitcast(I32)
@@ -85,7 +85,6 @@ def tile_moe_cas_mlp_relu_kernel(
             )
         for u in range(2):
             nc.sync.dma_start(w1_raw[u][:], w1_rows[:, :, u * H // 2 : (u + 1) * H // 2])
-        nc.sync.dma_start(w2_head[:], w2_rows[:, :, :P])
         nc.sync.dma_start(w2_rest[:], w2_rows[:, :, P:])
 
         gathered = {}
@@ -145,7 +144,7 @@ def tile_moe_cas_mlp_relu_kernel(
                 )
                 copy(result[t][:, tokens], y_acc[:])
 
-        def hidden(c, into):
+        def hidden(c, into, shared_relu=False):
             codes, plane = gathered[c]
             h_bf = placed("h_bf%d" % c, [P, CHUNK * PACK], BF16, H_AT + c * STAGE)
             for base in range(0, CHUNK, P):
@@ -161,7 +160,11 @@ def tile_moe_cas_mlp_relu_kernel(
                         stop=True,
                     )
                 dst = h_bf[:, base * PACK : (base + P) * PACK].rearrange("p (s j) -> p s j", j=PACK)
-                nc.scalar.activation(dst, h_acc[:].rearrange("p (j s) -> p s j", j=PACK), RELU)
+                sums = h_acc[:].rearrange("p (j s) -> p s j", j=PACK)
+                if shared_relu and base:
+                    nc.vector.tensor_scalar_max(dst, sums, 0.0)
+                else:
+                    nc.scalar.activation(dst, sums, RELU)
             slots = slice(c * CHUNK, (c + 1) * CHUNK)
             nc.vector.quantize_mx(
                 out=h_codes[:, slots].bitcast(FP8X4), scales=h_plane[:, slots], in_=h_bf[:]
@@ -191,6 +194,7 @@ def tile_moe_cas_mlp_relu_kernel(
 
         early = S - CHUNK
         early_codes = held("early_codes", [P, early], U32)
+        w2_bf = stage_w2(0, P, nc.scalar.copy, W2_AT)
         slot_plane = held("slot_plane", [P, S], U8)
         gather_scales(slot_plane[:], 0, S)
         gather_words(early_codes[:], 0, early)
@@ -199,14 +203,14 @@ def tile_moe_cas_mlp_relu_kernel(
             gathered[c] = (early_codes[:, slots], slot_plane[:, slots])
         prepare_w1()
         light(0, 0, (0, 1))
-        hidden(0, (2, 3))
-        w2_bf = stage_w2(0, P, nc.vector.tensor_copy, W1_AT + 1024)
-        light(0, 2 * BANK, (0, 1), nc.vector.tensor_copy)
-        quantize_w2(0, P, w2_bf, held("w2_codes0", [P, P], U32))
+        quantize_w2(0, P, w2_bf, placed("w2_codes0", [P, P], U32, W1_AT))
+        hidden(0, (2, 3), shared_relu=True)
         last_codes = placed("last_codes", [P, CHUNK], U32, H_AT)
         gather_words(last_codes[:], early, CHUNK)
         gathered[3] = (last_codes[:], slot_plane[:, early:])
+        light(0, 2 * BANK, (0,), nc.vector.tensor_copy)
         hidden(1, (4, 5))
+        light(0, 3 * BANK, (1,))
         heavy(0, 0, CHUNK, 6)
         scatter(0, 0, CHUNK)
         hidden(2, turn(2))

@@ -22,7 +22,7 @@ BANK = 512
 CHUNK = 256
 STRIPE = 16
 SPLIT = 24
-ROTATION = (7, 2, 3, 4, 5, 0, 1, 6)
+ROTATION = (0, 1, 2, 3, 4, 5, 6, 7)
 
 
 def tile_moe_cas_mlp_relu_kernel(
@@ -203,15 +203,15 @@ def tile_moe_cas_mlp_relu_kernel(
             gathered[c] = (early_codes[:, slots], slot_plane[:, slots])
         prepare_w1()
         light(0, 0, (0, 1))
+        light(0, 2 * BANK, (2,), nc.vector.tensor_copy)
+        light(0, 3 * BANK, (3,))
         quantize_w2(0, P, w2_bf, placed("w2_codes0", [P, P], U32, W1_AT))
-        hidden(0, (2, 3), shared_relu=True)
+        hidden(0, (4, 5), shared_relu=True)
         last_codes = placed("last_codes", [P, CHUNK], U32, H_AT)
         gather_words(last_codes[:], early, CHUNK)
         gathered[3] = (last_codes[:], slot_plane[:, early:])
-        light(0, 2 * BANK, (0,), nc.vector.tensor_copy)
-        hidden(1, (4, 5))
-        light(0, 3 * BANK, (1,))
-        heavy(0, 0, CHUNK, 6)
+        hidden(1, (6, 7))
+        heavy(0, 0, CHUNK, *turn(1))
         scatter(0, 0, CHUNK)
         hidden(2, turn(2))
         heavy(0, CHUNK, CHUNK, *turn(1))

@@ -22,7 +22,7 @@ BANK = 512
 CHUNK = 256
 STRIPE = 16
 SPLIT = 24
-ROTATION = (0, 1, 2, 3, 4, 5, 6, 7)
+ROTATION = (2, 3, 4, 5, 0, 1)
 
 
 def tile_moe_cas_mlp_relu_kernel(
@@ -146,7 +146,8 @@ def tile_moe_cas_mlp_relu_kernel(
 
         def hidden(c, into, shared_relu=False):
             codes, plane = gathered[c]
-            h_bf = placed("h_bf%d" % c, [P, CHUNK * PACK], BF16, H_AT + c * STAGE)
+            at = RAW_AT + T * 4 if c == 1 else H_AT + c * STAGE
+            h_bf = placed("h_bf%d" % c, [P, CHUNK * PACK], BF16, at)
             for base in range(0, CHUNK, P):
                 h_acc = banks[into[base // P]]
                 for j in range(PACK):
@@ -210,7 +211,7 @@ def tile_moe_cas_mlp_relu_kernel(
         last_codes = placed("last_codes", [P, CHUNK], U32, H_AT)
         gather_words(last_codes[:], early, CHUNK)
         gathered[3] = (last_codes[:], slot_plane[:, early:])
-        hidden(1, (6, 7))
+        hidden(1, (0, 1))
         heavy(0, 0, CHUNK, *turn(1))
         scatter(0, 0, CHUNK)
         hidden(2, turn(2))
@@ -219,13 +220,13 @@ def tile_moe_cas_mlp_relu_kernel(
         hidden(3, turn(2))
         heavy(0, 2 * CHUNK, CHUNK, *turn(1))
         scatter(0, 2 * CHUNK, CHUNK)
-        light(1, 0, turn(1))
+        light(1, 0, (6,))
         w2_bf = stage_w2(P, P, nc.scalar.copy, H_AT + 3 * STAGE)
         quantize_w2(P, P, w2_bf, held("w2_codes1", [P, P], U32))
         heavy(0, 3 * CHUNK, CHUNK, *turn(1))
         scatter(0, 3 * CHUNK, CHUNK)
         store(0)
-        light(1, BANK, turn(3))
+        light(1, BANK, [7] + turn(2))
         heavy(1, 0, CHUNK, *turn(1))
         scatter(1, 0, CHUNK)
         w2_bf = stage_w2(2 * P, 2 * P, nc.scalar.copy, H_AT + 3 * STAGE)

@@ -40,7 +40,7 @@ def tile_moe_cas_mlp_relu_kernel(
         def placed(name, shape, dtype, offset):
             return shared.tile(shape, dtype, name=name, align_bytes=64, offset=offset)
 
-        W1_AT, W2_AT, H_AT, STAGE, RAW_AT = 0, 4096, 8192, 2048, 16384
+        W1_AT, H_AT, STAGE, RAW_AT = 0, 8192, 2048, 16384
         offsets = keep.tile([P, S // STRIPE], U16)
         x_codes = held("x_codes", [P, T], I32)
         x_plane = held("x_plane", [P, T], U8)
@@ -72,8 +72,8 @@ def tile_moe_cas_mlp_relu_kernel(
         w1_rows = w1.rearrange("(p j) c -> p j c", j=PACK)
         w2_rows = w2.rearrange("(p j) c -> p j c", j=PACK)
         nc.sync.dma_start(offsets[:], offs)
-        nc.sync.dma_start(w_codes[:].bitcast(I32), w_words[0].bitcast(I32))
-        nc.sync.dma_start(w2_head[:], w2_rows[:, :, :P])
+        for half in (slice(0, N // 4), slice(N // 4, N // 2)):
+            nc.sync.dma_start(w_codes[:].bitcast(I32)[:, half], w_words[0].bitcast(I32)[:, half])
         for r in range(PACK):
             nc.sync.dma_start(
                 x_plane[r:P:32, :].bitcast(I32), x_scales[0, r:16:PACK, :].bitcast(I32)
@@ -85,6 +85,7 @@ def tile_moe_cas_mlp_relu_kernel(
             )
         for u in range(2):
             nc.sync.dma_start(w1_raw[u][:], w1_rows[:, :, u * H // 2 : (u + 1) * H // 2])
+        nc.sync.dma_start(w2_head[:], w2_rows[:, :, :P])
         nc.sync.dma_start(w2_rest[:], w2_rows[:, :, P:])
 
         gathered = {}
@@ -195,7 +196,6 @@ def tile_moe_cas_mlp_relu_kernel(
 
         early = S - CHUNK
         early_codes = held("early_codes", [P, early], U32)
-        w2_bf = stage_w2(0, P, nc.scalar.copy, W2_AT)
         slot_plane = held("slot_plane", [P, S], U8)
         gather_scales(slot_plane[:], 0, S)
         gather_words(early_codes[:], 0, early)
@@ -203,6 +203,7 @@ def tile_moe_cas_mlp_relu_kernel(
             slots = slice(c * CHUNK, (c + 1) * CHUNK)
             gathered[c] = (early_codes[:, slots], slot_plane[:, slots])
         prepare_w1()
+        w2_bf = stage_w2(0, P, nc.vector.tensor_copy, W1_AT + 1024)
         light(0, 0, (0, 1))
         light(0, 2 * BANK, (2,), nc.vector.tensor_copy)
         light(0, 3 * BANK, (3,))

@@ -15,14 +15,13 @@ FP8X4 = mybir.dt.float8_e4m3fn_x4
 FP4X4 = mybir.dt.float4_e2m1fn_x4
 COPY = mybir.ActivationFunctionType.Copy
 RELU = mybir.ActivationFunctionType.Relu
+ADD = mybir.AluOpType.add
+MULT = mybir.AluOpType.mult
 
 P = 128
 PACK = 4
 BANK = 512
-CHUNK = 256
 STRIPE = 16
-SPLIT = 24
-ROTATION = (2, 3, 4, 5, 0, 1)
 
 
 def tile_moe_cas_mlp_relu_kernel(
@@ -31,214 +30,201 @@ def tile_moe_cas_mlp_relu_kernel(
     nc = tc.nc
     with ExitStack() as ctx:
         keep = ctx.enter_context(tc.tile_pool(name="keep", bufs=1))
-        shared = ctx.enter_context(tc.tile_pool(name="shared", bufs=1))
         psum = ctx.enter_context(tc.psum_pool(name="psum", bufs=1))
 
         def held(name, shape, dtype):
             return keep.tile(shape, dtype, name=name, align_bytes=64)
 
-        def placed(name, shape, dtype, offset):
-            return shared.tile(shape, dtype, name=name, align_bytes=64, offset=offset)
-
-        W1_AT, H_AT, STAGE, RAW_AT = 0, 8192, 2048, 16384
         offsets = keep.tile([P, S // STRIPE], U16)
         x_codes = held("x_codes", [P, T], I32)
         x_plane = held("x_plane", [P, T], U8)
         w_codes = held("w_codes", [P, 2 * N], U8)
         w_plane = held("w_plane", [P, N], U8)
-        w1_raw = [
-            held("w1_raw0", [P, PACK, H // 2], F32),
-            placed("w1_raw1", [P, PACK, H // 2], F32, RAW_AT),
-        ]
+        w1_raw = [held("w1_raw%d" % u, [P, PACK, H // 2], F32) for u in range(2)]
         w2_head = held("w2_head", [P, PACK, P], F32)
         w2_rest = held("w2_rest", [P, PACK, N - P], F32)
+        w1_bf = held("w1_bf", [P, H * PACK], BF16)
         w1_codes = held("w1_codes", [P, H], U32)
         w1_plane = held("w1_plane", [P, H], U8)
+        w2_codes = held("w2_codes", [P, N], U32)
         w2_plane = held("w2_plane", [P, N], U8)
+        slot_plane = held("slot_plane", [P, S], U8)
         h_codes = held("h_codes", [P, S], U32)
         h_plane = held("h_plane", [P, S], U8)
+        zeros = held("zeros", [P, P], F32)
         z_rows = [held("z_rows%d" % t, [P, S], F32) for t in range(N // P)]
-        result = [placed("result%d" % t, [P, T], F32, RAW_AT + t * T * 4) for t in range(N // P)]
+        result = [held("result%d" % t, [P, T], F32) for t in range(N // P)]
         banks = [psum.tile([P, BANK], F32, name="bank%d" % b) for b in range(8)]
-        used = []
-
-        def turn(count):
-            first = len(used)
-            used.extend(range(count))
-            return [ROTATION[(first + b) % len(ROTATION)] for b in range(count)]
 
         nc.vector.memset(x_plane[:].bitcast(I32), 0)
         nc.gpsimd.memset(w_plane[:].bitcast(I32), 0)
+        nc.gpsimd.memset(zeros[:], 0.0)
         w1_rows = w1.rearrange("(p j) c -> p j c", j=PACK)
         w2_rows = w2.rearrange("(p j) c -> p j c", j=PACK)
+        x_rows = x_words[0].rearrange("p t d -> p (t d)").bitcast(I32)
+        nc.sync.dma_start(w1_raw[0][:], w1_rows[:, :, : H // 2])
         nc.sync.dma_start(offsets[:], offs)
-        for half in (slice(0, N // 4), slice(N // 4, N // 2)):
-            nc.sync.dma_start(w_codes[:].bitcast(I32)[:, half], w_words[0].bitcast(I32)[:, half])
         for r in range(PACK):
             nc.sync.dma_start(
                 x_plane[r:P:32, :].bitcast(I32), x_scales[0, r:16:PACK, :].bitcast(I32)
             )
-        nc.sync.dma_start(x_codes[:], x_words[0].rearrange("p t d -> p (t d)").bitcast(I32))
+        nc.sync.dma_start(w1_raw[1][:], w1_rows[:, :, H // 2 :])
+        nc.sync.dma_start(x_codes[:, : T // 2], x_rows[:, : T // 2])
+        nc.sync.dma_start(w_codes[:].bitcast(I32), w_words[0].bitcast(I32))
         for r in range(PACK):
             nc.sync.dma_start(
                 w_plane[r:P:32, :].bitcast(I32), w_scales[0, r:16:PACK, :].bitcast(I32)
             )
-        for u in range(2):
-            nc.sync.dma_start(w1_raw[u][:], w1_rows[:, :, u * H // 2 : (u + 1) * H // 2])
+        nc.sync.dma_start(x_codes[:, T // 2 :], x_rows[:, T // 2 :])
         nc.sync.dma_start(w2_head[:], w2_rows[:, :, :P])
         nc.sync.dma_start(w2_rest[:], w2_rows[:, :, P:])
 
-        gathered = {}
-        w2_codes = {}
+        slot_codes = {}
 
         def listed(first, count):
             return offsets[:, first // STRIPE : (first + count) // STRIPE]
 
-        def gather_words(codes, first, count):
-            nc.vector.tensor_copy(codes, x_codes[:].bitcast(U32).indirect(listed(first, count)))
+        def gather_words(first, count):
+            codes = held("slot_codes%d" % first, [P, count], U32)
+            nc.vector.tensor_copy(codes[:], x_codes[:].bitcast(U32).indirect(listed(first, count)))
+            for c in range(count // P):
+                slot_codes[first // P + c] = codes[:, c * P : (c + 1) * P]
 
-        def gather_scales(plane, first, count):
-            nc.vector.tensor_copy(plane, x_plane[:].indirect(listed(first, count)))
-
-        def prepare_w1():
-            w1_bf = placed("w1_bf", [P, H * PACK], BF16, W1_AT)
-            dst = w1_bf[:].rearrange("p (t m j) -> p m j t", t=PACK, j=PACK)
-            src = [raw[:].rearrange("p j (m t) -> p m j t", t=PACK) for raw in w1_raw]
-            half = P // 2
-            nc.scalar.activation(dst[:, :half], src[0], COPY)
-            nc.scalar.activation(dst[:, half : half + SPLIT], src[1][:, :SPLIT], COPY)
-            nc.vector.tensor_copy(dst[:, half + SPLIT :], src[1][:, SPLIT:])
-            for t in range(PACK):
-                cols = slice(t * P, (t + 1) * P)
-                nc.vector.quantize_mx(
-                    out=w1_codes[:, cols].bitcast(FP8X4),
-                    scales=w1_plane[:, cols],
-                    in_=w1_bf[:, t * H : (t + 1) * H],
-                )
-
-        def stage_w2(first, count, copy, offset):
-            raw = w2_head[:] if first == 0 else w2_rest[:, :, first - P : first - P + count]
-            w2_bf = placed("w2_bf%d" % first, [P, count * PACK], BF16, offset)
+        def stage_w2(first, count):
+            raw = w2_rest[:, :, first - P : first - P + count]
+            w2_bf = held("w2_bf%d" % first, [P, count * PACK], BF16)
             dst = w2_bf[:].rearrange("p (c i j) -> p c j i", i=4, j=PACK)
-            copy(dst, raw.rearrange("p j (c i) -> p c j i", i=4))
+            nc.scalar.copy(dst, raw.rearrange("p j (c i) -> p c j i", i=4))
             return w2_bf
 
-        def quantize_w2(first, count, w2_bf, codes):
+        def quantize_w2(first, count, w2_bf):
+            cols = slice(first, first + count)
             nc.vector.quantize_mx(
-                out=codes[:].bitcast(FP8X4), scales=w2_plane[:, first : first + count], in_=w2_bf[:]
+                out=w2_codes[:, cols].bitcast(FP8X4), scales=w2_plane[:, cols], in_=w2_bf[:]
             )
-            for t in range(count // P):
-                w2_codes[first // P + t] = codes[:, t * P : (t + 1) * P]
 
-        def light(t, start, into, copy=nc.scalar.copy):
-            for b, bank in enumerate(into):
-                tokens = slice(start + b * BANK, start + (b + 1) * BANK)
-                y_acc = banks[bank]
+        def light(t, quarter, bank, copy=nc.scalar.copy):
+            tokens = slice(quarter * BANK, (quarter + 1) * BANK)
+            y_acc = banks[bank]
+            nc.tensor.matmul_mx(
+                out=y_acc[:],
+                lhsT=w_codes[:, 2 * t * P : 2 * (t + 1) * P].bitcast(FP4X4),
+                lhsT_scale=w_plane[:, t * P : (t + 1) * P],
+                rhs=x_codes[:, tokens].bitcast(FP8X4),
+                rhs_scale=x_plane[:, tokens],
+                start=True,
+                stop=True,
+            )
+            copy(result[t][:, tokens], y_acc[:])
+
+        def hidden(c, bank):
+            slots = slice(c * P, (c + 1) * P)
+            h_acc = banks[bank]
+            for j in range(PACK):
                 nc.tensor.matmul_mx(
-                    out=y_acc[:],
-                    lhsT=w_codes[:, 2 * t * P : 2 * (t + 1) * P].bitcast(FP4X4),
-                    lhsT_scale=w_plane[:, t * P : (t + 1) * P],
-                    rhs=x_codes[:, tokens].bitcast(FP8X4),
-                    rhs_scale=x_plane[:, tokens],
+                    out=h_acc[:, j * P : (j + 1) * P],
+                    lhsT=w1_codes[:, j * P : (j + 1) * P].bitcast(FP8X4),
+                    lhsT_scale=w1_plane[:, j * P : (j + 1) * P],
+                    rhs=slot_codes[c].bitcast(FP8X4),
+                    rhs_scale=slot_plane[:, slots],
                     start=True,
                     stop=True,
                 )
-                copy(result[t][:, tokens], y_acc[:])
-
-        def hidden(c, into, shared_relu=False):
-            codes, plane = gathered[c]
-            at = RAW_AT + T * 4 if c == 1 else H_AT + c * STAGE
-            h_bf = placed("h_bf%d" % c, [P, CHUNK * PACK], BF16, at)
-            for base in range(0, CHUNK, P):
-                h_acc = banks[into[base // P]]
-                for j in range(PACK):
-                    nc.tensor.matmul_mx(
-                        out=h_acc[:, j * P : (j + 1) * P],
-                        lhsT=w1_codes[:, j * P : (j + 1) * P].bitcast(FP8X4),
-                        lhsT_scale=w1_plane[:, j * P : (j + 1) * P],
-                        rhs=codes[:, base : base + P].bitcast(FP8X4),
-                        rhs_scale=plane[:, base : base + P],
-                        start=True,
-                        stop=True,
-                    )
-                dst = h_bf[:, base * PACK : (base + P) * PACK].rearrange("p (s j) -> p s j", j=PACK)
-                sums = h_acc[:].rearrange("p (j s) -> p s j", j=PACK)
-                if shared_relu and base:
-                    nc.vector.tensor_scalar_max(dst, sums, 0.0)
-                else:
-                    nc.scalar.activation(dst, sums, RELU)
-            slots = slice(c * CHUNK, (c + 1) * CHUNK)
+            h_bf = held("h_bf%d" % c, [P, P * PACK], BF16)
+            nc.scalar.activation(
+                h_bf[:].rearrange("p (s j) -> p s j", j=PACK),
+                h_acc[:].rearrange("p (j s) -> p s j", j=PACK),
+                RELU,
+            )
             nc.vector.quantize_mx(
                 out=h_codes[:, slots].bitcast(FP8X4), scales=h_plane[:, slots], in_=h_bf[:]
             )
 
-        def heavy(t, first, count, bank):
-            slots = slice(first, first + count)
+        def heavy(t, first, widths, bank):
             z_acc = banks[bank]
-            nc.tensor.matmul_mx(
-                out=z_acc[:, :count],
-                lhsT=w2_codes[t].bitcast(FP8X4),
-                lhsT_scale=w2_plane[:, t * P : (t + 1) * P],
-                rhs=h_codes[:, slots].bitcast(FP8X4),
-                rhs_scale=h_plane[:, slots],
-                start=True,
-                stop=True,
-            )
-            nc.scalar.copy(z_rows[t][:, slots], z_acc[:, :count])
+            at = 0
+            for count in widths:
+                slots = slice(first + at, first + at + count)
+                nc.tensor.matmul_mx(
+                    out=z_acc[:, at : at + count],
+                    lhsT=w2_codes[:, t * P : (t + 1) * P].bitcast(FP8X4),
+                    lhsT_scale=w2_plane[:, t * P : (t + 1) * P],
+                    rhs=h_codes[:, slots].bitcast(FP8X4),
+                    rhs_scale=h_plane[:, slots],
+                    start=True,
+                    stop=True,
+                )
+                at += count
+            nc.scalar.copy(z_rows[t][:, first : first + at], z_acc[:, :at])
 
         def scatter(t, first, count):
-            nc.vector.tensor_copy(
-                result[t][:].indirect(listed(first, count)), z_rows[t][:, first : first + count]
-            )
+            window = result[t][:].indirect(listed(first, count))
+            values = z_rows[t][:, first : first + count]
+            if count == P:
+                nc.vector.tensor_tensor(window, values, zeros[:], ADD)
+            else:
+                nc.vector.tensor_copy(window, values)
 
         def store(t):
             nc.sync.dma_start(out[t * P : (t + 1) * P, :], result[t][:])
 
-        early = S - CHUNK
-        early_codes = held("early_codes", [P, early], U32)
-        slot_plane = held("slot_plane", [P, S], U8)
-        gather_scales(slot_plane[:], 0, S)
-        gather_words(early_codes[:], 0, early)
-        for c in range(early // CHUNK):
-            slots = slice(c * CHUNK, (c + 1) * CHUNK)
-            gathered[c] = (early_codes[:, slots], slot_plane[:, slots])
-        prepare_w1()
-        w2_bf = stage_w2(0, P, nc.vector.tensor_copy, W1_AT + 1024)
-        light(0, 0, (0, 1))
-        light(0, 2 * BANK, (2,), nc.vector.tensor_copy)
-        light(0, 3 * BANK, (3,))
-        quantize_w2(0, P, w2_bf, placed("w2_codes0", [P, P], U32, W1_AT))
-        hidden(0, (4, 5), shared_relu=True)
-        last_codes = placed("last_codes", [P, CHUNK], U32, H_AT)
-        gather_words(last_codes[:], early, CHUNK)
-        gathered[3] = (last_codes[:], slot_plane[:, early:])
-        hidden(1, (0, 1))
-        heavy(0, 0, CHUNK, *turn(1))
-        scatter(0, 0, CHUNK)
-        hidden(2, turn(2))
-        heavy(0, CHUNK, CHUNK, *turn(1))
-        scatter(0, CHUNK, CHUNK)
-        hidden(3, turn(2))
-        heavy(0, 2 * CHUNK, CHUNK, *turn(1))
-        scatter(0, 2 * CHUNK, CHUNK)
-        light(1, 0, (6,))
-        w2_bf = stage_w2(P, P, nc.scalar.copy, H_AT + 3 * STAGE)
-        quantize_w2(P, P, w2_bf, held("w2_codes1", [P, P], U32))
-        heavy(0, 3 * CHUNK, CHUNK, *turn(1))
-        scatter(0, 3 * CHUNK, CHUNK)
+        nc.vector.tensor_copy(slot_plane[:], x_plane[:].indirect(offsets[:]))
+        grouped = w1_bf[:].rearrange("p (t m j) -> p m j t", t=PACK, j=PACK)
+        for u in range(2):
+            nc.scalar.activation(
+                grouped[:, u * P // 2 : (u + 1) * P // 2],
+                w1_raw[u][:].rearrange("p j (m t) -> p m j t", t=PACK),
+                COPY,
+            )
+        nc.vector.quantize_mx(out=w1_codes[:].bitcast(FP8X4), scales=w1_plane[:], in_=w1_bf[:])
+        for quarter in range(3):
+            light(0, quarter, quarter)
+        gather_words(0, 2 * P)
+        gather_words(2 * P, 2 * P)
+        gather_words(4 * P, 4 * P)
+        head_bf = held("head_bf", [P, P * PACK], BF16)
+        nc.gpsimd.tensor_scalar(
+            head_bf[:].rearrange("p (c j) -> p c j", j=PACK),
+            w2_head[:].rearrange("p j c -> p c j"),
+            1.0,
+            0.0,
+            MULT,
+            ADD,
+        )
+        quantize_w2(0, P, head_bf)
+        hidden(0, 3)
+        hidden(1, 4)
+        light(0, 3, 3, nc.vector.tensor_copy)
+        hidden(2, 5)
+        heavy(0, 0, [P], 6)
+        scatter(0, 0, P)
+        hidden(3, 7)
+        heavy(0, P, [P], 0)
+        scatter(0, P, P)
+        hidden(4, 4)
+        heavy(0, 2 * P, [P], 1)
+        scatter(0, 2 * P, P)
+        hidden(5, 5)
+        hidden(6, 6)
+        hidden(7, 7)
+        heavy(0, 3 * P, [2 * P], 2)
+        scatter(0, 3 * P, 2 * P)
+        quantize_w2(P, P, stage_w2(P, P))
+        heavy(0, 5 * P, [2 * P, P], 0)
+        scatter(0, 5 * P, 3 * P)
         store(0)
-        light(1, BANK, [7] + turn(2))
-        heavy(1, 0, CHUNK, *turn(1))
-        scatter(1, 0, CHUNK)
-        w2_bf = stage_w2(2 * P, 2 * P, nc.scalar.copy, H_AT + 3 * STAGE)
-        quantize_w2(2 * P, 2 * P, w2_bf, held("w2_codes2", [P, 2 * P], U32))
-        heavy(1, CHUNK, CHUNK, *turn(1))
-        heavy(1, BANK, BANK, *turn(1))
-        scatter(1, CHUNK, early)
+        for quarter in range(4):
+            light(1, quarter, 4 + quarter)
+        heavy(1, 0, [BANK], 1)
+        scatter(1, 0, BANK)
+        quantize_w2(2 * P, 2 * P, stage_w2(2 * P, 2 * P))
+        heavy(1, BANK, [BANK], 2)
+        scatter(1, BANK, BANK)
         store(1)
         for t in range(2, N // P):
-            light(t, 0, turn(4))
-            heavy(t, 0, BANK, *turn(1))
-            heavy(t, BANK, BANK, *turn(1))
+            for quarter in range(4):
+                light(t, quarter, 4 + quarter)
+            heavy(t, 0, [BANK], 0 + 2 * (t - 2))
+            heavy(t, BANK, [BANK], 1 + 2 * (t - 2))
             scatter(t, 0, S)
             store(t)

@@ -22,6 +22,7 @@ P = 128
 PACK = 4
 BANK = 512
 STRIPE = 16
+SCALAR_GROUPS = 80
 
 
 def tile_moe_cas_mlp_relu_kernel(
@@ -40,7 +41,7 @@ def tile_moe_cas_mlp_relu_kernel(
         x_plane = held("x_plane", [P, T], U8)
         w_codes = held("w_codes", [P, 2 * N], U8)
         w_plane = held("w_plane", [P, N], U8)
-        w1_raw = [held("w1_raw%d" % u, [P, PACK, H // 2], F32) for u in range(2)]
+        w1_raw = held("w1_raw", [P, PACK, H], F32)
         w2_head = held("w2_head", [P, PACK, P], F32)
         w2_rest = held("w2_rest", [P, PACK, N - P], F32)
         w1_bf = held("w1_bf", [P, H * PACK], BF16)
@@ -59,16 +60,17 @@ def tile_moe_cas_mlp_relu_kernel(
         nc.vector.memset(x_plane[:].bitcast(I32), 0)
         nc.gpsimd.memset(w_plane[:].bitcast(I32), 0)
         nc.gpsimd.memset(zeros[:], 0.0)
+        nc.scalar.activation(zeros[:, :1], zeros[:, :1], RELU)
         w1_rows = w1.rearrange("(p j) c -> p j c", j=PACK)
         w2_rows = w2.rearrange("(p j) c -> p j c", j=PACK)
         x_rows = x_words[0].rearrange("p t d -> p (t d)").bitcast(I32)
-        nc.sync.dma_start(w1_raw[0][:], w1_rows[:, :, : H // 2])
+        nc.sync.dma_start(w1_raw[:, : PACK // 2], w1_rows[:, : PACK // 2])
         nc.sync.dma_start(offsets[:], offs)
         for r in range(PACK):
             nc.sync.dma_start(
                 x_plane[r:P:32, :].bitcast(I32), x_scales[0, r:16:PACK, :].bitcast(I32)
             )
-        nc.sync.dma_start(w1_raw[1][:], w1_rows[:, :, H // 2 :])
+        nc.sync.dma_start(w1_raw[:, PACK // 2 :], w1_rows[:, PACK // 2 :])
         nc.sync.dma_start(x_codes[:, : T // 2], x_rows[:, : T // 2])
         nc.sync.dma_start(w_codes[:].bitcast(I32), w_words[0].bitcast(I32))
         for r in range(PACK):
@@ -170,12 +172,9 @@ def tile_moe_cas_mlp_relu_kernel(
 
         nc.vector.tensor_copy(slot_plane[:], x_plane[:].indirect(offsets[:]))
         grouped = w1_bf[:].rearrange("p (t m j) -> p m j t", t=PACK, j=PACK)
-        for u in range(2):
-            nc.scalar.activation(
-                grouped[:, u * P // 2 : (u + 1) * P // 2],
-                w1_raw[u][:].rearrange("p j (m t) -> p m j t", t=PACK),
-                COPY,
-            )
+        source = w1_raw[:].rearrange("p j (m t) -> p m j t", t=PACK)
+        nc.scalar.activation(grouped[:, :SCALAR_GROUPS], source[:, :SCALAR_GROUPS], COPY)
+        nc.vector.tensor_copy(grouped[:, SCALAR_GROUPS:], source[:, SCALAR_GROUPS:])
         nc.vector.quantize_mx(out=w1_codes[:].bitcast(FP8X4), scales=w1_plane[:], in_=w1_bf[:])
         for quarter in range(3):
             light(0, quarter, quarter)

@@ -209,16 +209,18 @@ def tile_moe_cas_mlp_relu_kernel(
         heavy(0, 3 * P, [2 * P], 2)
         scatter(0, 3 * P, 2 * P)
         quantize_w2(P, P, stage_w2(P, P))
+        light(1, 0, 4)
         heavy(0, 5 * P, [2 * P, P], 0)
         scatter(0, 5 * P, 3 * P)
         store(0)
-        for quarter in range(4):
+        for quarter in range(1, 4):
             light(1, quarter, 4 + quarter)
-        heavy(1, 0, [BANK], 1)
-        scatter(1, 0, BANK)
+        heavy(1, 0, [2 * P], 1)
+        scatter(1, 0, 2 * P)
+        heavy(1, 2 * P, [2 * P], 2)
         quantize_w2(2 * P, 2 * P, stage_w2(2 * P, 2 * P))
-        heavy(1, BANK, [BANK], 2)
-        scatter(1, BANK, BANK)
+        heavy(1, BANK, [BANK], 3)
+        scatter(1, 2 * P, 6 * P)
         store(1)
         for t in range(2, N // P):
             for quarter in range(4):

@@ -119,25 +119,29 @@ def tile_moe_cas_mlp_relu_kernel(
             )
             copy(result[t][:, tokens], y_acc[:])
 
-        def hidden(c, bank):
-            slots = slice(c * P, (c + 1) * P)
-            h_acc = banks[bank]
-            for j in range(PACK):
-                nc.tensor.matmul_mx(
-                    out=h_acc[:, j * P : (j + 1) * P],
-                    lhsT=w1_codes[:, j * P : (j + 1) * P].bitcast(FP8X4),
-                    lhsT_scale=w1_plane[:, j * P : (j + 1) * P],
-                    rhs=slot_codes[c].bitcast(FP8X4),
-                    rhs_scale=slot_plane[:, slots],
-                    start=True,
-                    stop=True,
+        def hidden(first, into):
+            count = len(into) * P
+            h_bf = held("h_bf%d" % first, [P, count * PACK], BF16)
+            for part, bank in enumerate(into):
+                c = first // P + part
+                h_acc = banks[bank]
+                for j in range(PACK):
+                    nc.tensor.matmul_mx(
+                        out=h_acc[:, j * P : (j + 1) * P],
+                        lhsT=w1_codes[:, j * P : (j + 1) * P].bitcast(FP8X4),
+                        lhsT_scale=w1_plane[:, j * P : (j + 1) * P],
+                        rhs=slot_codes[c].bitcast(FP8X4),
+                        rhs_scale=slot_plane[:, c * P : (c + 1) * P],
+                        start=True,
+                        stop=True,
+                    )
+                staged = h_bf[:, part * P * PACK : (part + 1) * P * PACK]
+                nc.scalar.activation(
+                    staged.rearrange("p (s j) -> p s j", j=PACK),
+                    h_acc[:].rearrange("p (j s) -> p s j", j=PACK),
+                    RELU,
                 )
-            h_bf = held("h_bf%d" % c, [P, P * PACK], BF16)
-            nc.scalar.activation(
-                h_bf[:].rearrange("p (s j) -> p s j", j=PACK),
-                h_acc[:].rearrange("p (j s) -> p s j", j=PACK),
-                RELU,
-            )
+            slots = slice(first, first + count)
             nc.vector.quantize_mx(
                 out=h_codes[:, slots].bitcast(FP8X4), scales=h_plane[:, slots], in_=h_bf[:]
             )
@@ -191,41 +195,39 @@ def tile_moe_cas_mlp_relu_kernel(
             ADD,
         )
         quantize_w2(0, P, head_bf)
-        hidden(0, 3)
-        hidden(1, 4)
+        hidden(0, (3,))
+        hidden(P, (4,))
         light(0, 3, 3, nc.vector.tensor_copy)
-        hidden(2, 5)
         heavy(0, 0, [P], 6)
         scatter(0, 0, P)
-        hidden(3, 7)
+        hidden(2 * P, (5, 7))
         heavy(0, P, [P], 0)
         scatter(0, P, P)
-        hidden(4, 4)
-        heavy(0, 2 * P, [P], 1)
-        scatter(0, 2 * P, P)
-        hidden(5, 5)
-        hidden(6, 6)
-        hidden(7, 7)
-        heavy(0, 3 * P, [2 * P], 2)
-        scatter(0, 3 * P, 2 * P)
+        hidden(4 * P, (4, 5))
+        heavy(0, 2 * P, [2 * P], 1)
+        scatter(0, 2 * P, 2 * P)
+        hidden(6 * P, (6, 7))
+        heavy(0, 4 * P, [2 * P], 2)
+        scatter(0, 4 * P, 2 * P)
         quantize_w2(P, P, stage_w2(P, P))
-        light(1, 0, 4)
-        heavy(0, 5 * P, [2 * P, P], 0)
-        scatter(0, 5 * P, 3 * P)
+        light(1, 0, 3)
+        light(1, 1, 4)
+        heavy(0, 6 * P, [2 * P], 0)
+        scatter(0, 6 * P, 2 * P)
         store(0)
-        for quarter in range(1, 4):
-            light(1, quarter, 4 + quarter)
+        light(1, 2, 5)
+        light(1, 3, 6)
         heavy(1, 0, [2 * P], 1)
         scatter(1, 0, 2 * P)
         heavy(1, 2 * P, [2 * P], 2)
         quantize_w2(2 * P, 2 * P, stage_w2(2 * P, 2 * P))
-        heavy(1, BANK, [BANK], 3)
+        heavy(1, BANK, [BANK], 7)
         scatter(1, 2 * P, 6 * P)
         store(1)
         for t in range(2, N // P):
             for quarter in range(4):
-                light(t, quarter, 4 + quarter)
-            heavy(t, 0, [BANK], 0 + 2 * (t - 2))
-            heavy(t, BANK, [BANK], 1 + 2 * (t - 2))
+                light(t, quarter, 3 + quarter)
+            heavy(t, 0, [BANK], (0, 2)[t - 2])
+            heavy(t, BANK, [BANK], (1, 7)[t - 2])
             scatter(t, 0, S)
             store(t)

@@ -72,7 +72,8 @@ def tile_moe_cas_mlp_relu_kernel(
             )
         nc.sync.dma_start(w1_raw[:, PACK // 2 :], w1_rows[:, PACK // 2 :])
         nc.sync.dma_start(x_codes[:, : T // 2], x_rows[:, : T // 2])
-        nc.sync.dma_start(w_codes[:].bitcast(I32), w_words[0].bitcast(I32))
+        w_rows = w_words[0].bitcast(I32)
+        nc.sync.dma_start(w_codes[:].bitcast(I32)[:, : P // 2], w_rows[:, : P // 2])
         for r in range(PACK):
             nc.sync.dma_start(
                 w_plane[r:P:32, :].bitcast(I32), w_scales[0, r:16:PACK, :].bitcast(I32)
@@ -80,6 +81,7 @@ def tile_moe_cas_mlp_relu_kernel(
         nc.sync.dma_start(x_codes[:, T // 2 :], x_rows[:, T // 2 :])
         nc.sync.dma_start(w2_head[:], w2_rows[:, :, :P])
         nc.sync.dma_start(w2_rest[:], w2_rows[:, :, P:])
+        nc.sync.dma_start(w_codes[:].bitcast(I32)[:, P // 2 :], w_rows[:, P // 2 :])
 
         slot_codes = {}
 

@@ -22,7 +22,6 @@ P = 128
 PACK = 4
 BANK = 512
 STRIPE = 16
-SCALAR_GROUPS = 80
 
 
 def tile_moe_cas_mlp_relu_kernel(
@@ -41,7 +40,7 @@ def tile_moe_cas_mlp_relu_kernel(
         x_plane = held("x_plane", [P, T], U8)
         w_codes = held("w_codes", [P, 2 * N], U8)
         w_plane = held("w_plane", [P, N], U8)
-        w1_raw = held("w1_raw", [P, PACK, H], F32)
+        w1_raw = [held("w1_raw%d" % u, [P, PACK, H // 2], F32) for u in range(2)]
         w2_head = held("w2_head", [P, PACK, P], F32)
         w2_rest = held("w2_rest", [P, PACK, N - P], F32)
         w1_bf = held("w1_bf", [P, H * PACK], BF16)
@@ -60,17 +59,16 @@ def tile_moe_cas_mlp_relu_kernel(
         nc.vector.memset(x_plane[:].bitcast(I32), 0)
         nc.gpsimd.memset(w_plane[:].bitcast(I32), 0)
         nc.gpsimd.memset(zeros[:], 0.0)
-        nc.scalar.activation(zeros[:, :1], zeros[:, :1], RELU)
         w1_rows = w1.rearrange("(p j) c -> p j c", j=PACK)
         w2_rows = w2.rearrange("(p j) c -> p j c", j=PACK)
         x_rows = x_words[0].rearrange("p t d -> p (t d)").bitcast(I32)
-        nc.sync.dma_start(w1_raw[:, : PACK // 2], w1_rows[:, : PACK // 2])
+        nc.sync.dma_start(w1_raw[0][:], w1_rows[:, :, : H // 2])
         nc.sync.dma_start(offsets[:], offs)
         for r in range(PACK):
             nc.sync.dma_start(
                 x_plane[r:P:32, :].bitcast(I32), x_scales[0, r:16:PACK, :].bitcast(I32)
             )
-        nc.sync.dma_start(w1_raw[:, PACK // 2 :], w1_rows[:, PACK // 2 :])
+        nc.sync.dma_start(w1_raw[1][:], w1_rows[:, :, H // 2 :])
         nc.sync.dma_start(x_codes[:, : T // 2], x_rows[:, : T // 2])
         w_rows = w_words[0].bitcast(I32)
         nc.sync.dma_start(w_codes[:].bitcast(I32)[:, : P // 2], w_rows[:, : P // 2])
@@ -178,9 +176,12 @@ def tile_moe_cas_mlp_relu_kernel(
 
         nc.vector.tensor_copy(slot_plane[:], x_plane[:].indirect(offsets[:]))
         grouped = w1_bf[:].rearrange("p (t m j) -> p m j t", t=PACK, j=PACK)
-        source = w1_raw[:].rearrange("p j (m t) -> p m j t", t=PACK)
-        nc.scalar.activation(grouped[:, :SCALAR_GROUPS], source[:, :SCALAR_GROUPS], COPY)
-        nc.vector.tensor_copy(grouped[:, SCALAR_GROUPS:], source[:, SCALAR_GROUPS:])
+        for u in range(2):
+            nc.scalar.activation(
+                grouped[:, u * P // 2 : (u + 1) * P // 2],
+                w1_raw[u][:].rearrange("p j (m t) -> p m j t", t=PACK),
+                COPY,
+            )
         nc.vector.quantize_mx(out=w1_codes[:].bitcast(FP8X4), scales=w1_plane[:], in_=w1_bf[:])
         for quarter in range(3):
             light(0, quarter, quarter)

@@ -30,6 +30,7 @@ def tile_moe_cas_mlp_relu_kernel(
     nc = tc.nc
     with ExitStack() as ctx:
         keep = ctx.enter_context(tc.tile_pool(name="keep", bufs=1))
+        reused = ctx.enter_context(tc.tile_pool(name="reused", bufs=1))
         psum = ctx.enter_context(tc.psum_pool(name="psum", bufs=1))
 
         def held(name, shape, dtype):
@@ -38,11 +39,10 @@ def tile_moe_cas_mlp_relu_kernel(
         offsets = keep.tile([P, S // STRIPE], U16)
         x_codes = held("x_codes", [P, T], I32)
         x_plane = held("x_plane", [P, T], U8)
-        w_codes = held("w_codes", [P, 2 * N], U8)
+        w_head = held("w_head", [P, 2 * P], U8)
         w_plane = held("w_plane", [P, N], U8)
         w1_raw = [held("w1_raw%d" % u, [P, PACK, H // 2], F32) for u in range(2)]
-        w2_head = held("w2_head", [P, PACK, P], F32)
-        w2_rest = held("w2_rest", [P, PACK, N - P], F32)
+        w2_raw = [held("w2_raw%d" % u, [P, PACK, c], F32) for u, c in enumerate((P, P, 2 * P))]
         w1_bf = held("w1_bf", [P, H * PACK], BF16)
         w1_codes = held("w1_codes", [P, H], U32)
         w1_plane = held("w1_plane", [P, H], U8)
@@ -55,6 +55,16 @@ def tile_moe_cas_mlp_relu_kernel(
         z_rows = [held("z_rows%d" % t, [P, S], F32) for t in range(N // P)]
         result = [held("result%d" % t, [P, T], F32) for t in range(N // P)]
         banks = [psum.tile([P, BANK], F32, name="bank%d" % b) for b in range(8)]
+        WORDS = P * PACK
+        h_first = held("h_first", [P, WORDS], BF16)
+        h_12 = reused.tile([P, 2 * WORDS], BF16, name="h_12", align_bytes=64, offset=0)
+        w_rest = reused.tile([P, 2 * (N - P)], U8, name="w_rest", align_bytes=64, offset=0)
+        h_34 = held("h_34", [P, 2 * WORDS], BF16)
+        h_56 = held("h_56", [P, 2 * WORDS], BF16)
+        h_last = held("h_last", [P, WORDS], BF16)
+        w2_bf1 = held("w2_bf1", [P, WORDS], BF16)
+        staged = [h_first[:], h_12[:, :WORDS], h_12[:, WORDS:], h_34[:, :WORDS], h_34[:, WORDS:],
+                  h_56[:, :WORDS], h_56[:, WORDS:], h_last[:]]
 
         nc.vector.memset(x_plane[:].bitcast(I32), 0)
         nc.gpsimd.memset(w_plane[:].bitcast(I32), 0)
@@ -71,15 +81,15 @@ def tile_moe_cas_mlp_relu_kernel(
         nc.sync.dma_start(w1_raw[1][:], w1_rows[:, :, H // 2 :])
         nc.sync.dma_start(x_codes[:, : T // 2], x_rows[:, : T // 2])
         w_rows = w_words[0].bitcast(I32)
-        nc.sync.dma_start(w_codes[:].bitcast(I32)[:, : P // 2], w_rows[:, : P // 2])
+        nc.sync.dma_start(w_head[:].bitcast(I32), w_rows[:, : P // 2])
         for r in range(PACK):
             nc.sync.dma_start(
                 w_plane[r:P:32, :].bitcast(I32), w_scales[0, r:16:PACK, :].bitcast(I32)
             )
         nc.sync.dma_start(x_codes[:, T // 2 :], x_rows[:, T // 2 :])
-        nc.sync.dma_start(w2_head[:], w2_rows[:, :, :P])
-        nc.sync.dma_start(w2_rest[:], w2_rows[:, :, P:])
-        nc.sync.dma_start(w_codes[:].bitcast(I32)[:, P // 2 :], w_rows[:, P // 2 :])
+        nc.sync.dma_start(w2_raw[0][:], w2_rows[:, :, :P])
+        nc.sync.dma_start(w2_raw[1][:], w2_rows[:, :, P : 2 * P])
+        nc.sync.dma_start(w2_raw[2][:], w2_rows[:, :, 2 * P :])
 
         slot_codes = {}
 
@@ -92,25 +102,29 @@ def tile_moe_cas_mlp_relu_kernel(
             for c in range(count // P):
                 slot_codes[first // P + c] = codes[:, c * P : (c + 1) * P]
 
-        def stage_w2(first, count):
-            raw = w2_rest[:, :, first - P : first - P + count]
-            w2_bf = held("w2_bf%d" % first, [P, count * PACK], BF16)
-            dst = w2_bf[:].rearrange("p (c i j) -> p c j i", i=4, j=PACK)
-            nc.scalar.copy(dst, raw.rearrange("p j (c i) -> p c j i", i=4))
-            return w2_bf
+        def cast_w2(raw, w2_bf):
+            nc.gpsimd.tensor_scalar(
+                w2_bf.rearrange("p (c j) -> p c j", j=PACK),
+                raw[:].rearrange("p j c -> p c j"),
+                1.0,
+                0.0,
+                MULT,
+                ADD,
+            )
 
         def quantize_w2(first, count, w2_bf):
             cols = slice(first, first + count)
             nc.vector.quantize_mx(
-                out=w2_codes[:, cols].bitcast(FP8X4), scales=w2_plane[:, cols], in_=w2_bf[:]
+                out=w2_codes[:, cols].bitcast(FP8X4), scales=w2_plane[:, cols], in_=w2_bf
             )
 
         def light(t, quarter, bank, copy=nc.scalar.copy):
             tokens = slice(quarter * BANK, (quarter + 1) * BANK)
             y_acc = banks[bank]
+            w_cols = w_head[:] if t == 0 else w_rest[:, 2 * (t - 1) * P : 2 * t * P]
             nc.tensor.matmul_mx(
                 out=y_acc[:],
-                lhsT=w_codes[:, 2 * t * P : 2 * (t + 1) * P].bitcast(FP4X4),
+                lhsT=w_cols.bitcast(FP4X4),
                 lhsT_scale=w_plane[:, t * P : (t + 1) * P],
                 rhs=x_codes[:, tokens].bitcast(FP8X4),
                 rhs_scale=x_plane[:, tokens],
@@ -119,31 +133,29 @@ def tile_moe_cas_mlp_relu_kernel(
             )
             copy(result[t][:, tokens], y_acc[:])
 
-        def hidden(first, into):
-            count = len(into) * P
-            h_bf = held("h_bf%d" % first, [P, count * PACK], BF16)
-            for part, bank in enumerate(into):
-                c = first // P + part
-                h_acc = banks[bank]
-                for j in range(PACK):
-                    nc.tensor.matmul_mx(
-                        out=h_acc[:, j * P : (j + 1) * P],
-                        lhsT=w1_codes[:, j * P : (j + 1) * P].bitcast(FP8X4),
-                        lhsT_scale=w1_plane[:, j * P : (j + 1) * P],
-                        rhs=slot_codes[c].bitcast(FP8X4),
-                        rhs_scale=slot_plane[:, c * P : (c + 1) * P],
-                        start=True,
-                        stop=True,
-                    )
-                staged = h_bf[:, part * P * PACK : (part + 1) * P * PACK]
-                nc.scalar.activation(
-                    staged.rearrange("p (s j) -> p s j", j=PACK),
-                    h_acc[:].rearrange("p (j s) -> p s j", j=PACK),
-                    RELU,
+        def hidden(c, bank, on_vector=False):
+            h_acc = banks[bank]
+            for j in range(PACK):
+                nc.tensor.matmul_mx(
+                    out=h_acc[:, j * P : (j + 1) * P],
+                    lhsT=w1_codes[:, j * P : (j + 1) * P].bitcast(FP8X4),
+                    lhsT_scale=w1_plane[:, j * P : (j + 1) * P],
+                    rhs=slot_codes[c].bitcast(FP8X4),
+                    rhs_scale=slot_plane[:, c * P : (c + 1) * P],
+                    start=True,
+                    stop=True,
                 )
+            dst = staged[c].rearrange("p (s j) -> p s j", j=PACK)
+            src = h_acc[:].rearrange("p (j s) -> p s j", j=PACK)
+            if on_vector:
+                nc.vector.tensor_scalar_max(dst, src, 0.0)
+            else:
+                nc.scalar.activation(dst, src, RELU)
+
+        def quantize_h(first, count, h_bf):
             slots = slice(first, first + count)
             nc.vector.quantize_mx(
-                out=h_codes[:, slots].bitcast(FP8X4), scales=h_plane[:, slots], in_=h_bf[:]
+                out=h_codes[:, slots].bitcast(FP8X4), scales=h_plane[:, slots], in_=h_bf
             )
 
         def heavy(t, first, widths, bank):
@@ -183,54 +195,46 @@ def tile_moe_cas_mlp_relu_kernel(
                 COPY,
             )
         nc.vector.quantize_mx(out=w1_codes[:].bitcast(FP8X4), scales=w1_plane[:], in_=w1_bf[:])
-        for quarter in range(3):
-            light(0, quarter, quarter)
+        light(0, 0, 0)
+        light(0, 1, 1)
         gather_words(0, 2 * P)
         gather_words(2 * P, 2 * P)
         gather_words(4 * P, 4 * P)
-        head_bf = held("head_bf", [P, P * PACK], BF16)
-        nc.gpsimd.tensor_scalar(
-            head_bf[:].rearrange("p (c j) -> p c j", j=PACK),
-            w2_head[:].rearrange("p j c -> p c j"),
-            1.0,
-            0.0,
-            MULT,
-            ADD,
-        )
-        quantize_w2(0, P, head_bf)
-        hidden(0, (3,))
-        hidden(P, (4,))
-        light(0, 3, 3, nc.vector.tensor_copy)
-        heavy(0, 0, [P], 6)
+        cast_w2(w2_raw[0], staged[2])
+        quantize_w2(0, P, staged[2])
+        cast_w2(w2_raw[1], w2_bf1[:])
+        hidden(0, 2)
+        quantize_h(0, P, h_first[:])
+        hidden(1, 3)
+        light(0, 2, 1)
+        hidden(2, 4, on_vector=True)
+        light(0, 3, 2, nc.vector.tensor_copy)
+        heavy(0, 0, [P], 0)
+        quantize_h(P, 2 * P, h_12[:])
+        nc.sync.dma_start(w_rest[:].bitcast(I32), w_rows[:, P // 2 :])
         scatter(0, 0, P)
-        hidden(2 * P, (5, 7))
-        heavy(0, P, [P], 0)
-        scatter(0, P, P)
-        hidden(4 * P, (4, 5))
-        heavy(0, 2 * P, [2 * P], 1)
-        scatter(0, 2 * P, 2 * P)
-        hidden(6 * P, (6, 7))
-        heavy(0, 4 * P, [2 * P], 2)
-        scatter(0, 4 * P, 2 * P)
-        quantize_w2(P, P, stage_w2(P, P))
-        light(1, 0, 3)
-        light(1, 1, 4)
-        heavy(0, 6 * P, [2 * P], 0)
-        scatter(0, 6 * P, 2 * P)
+        hidden(3, 3)
+        hidden(4, 4)
+        heavy(0, P, [2 * P], 5)
+        quantize_h(3 * P, 2 * P, h_34[:])
+        quantize_w2(P, P, w2_bf1[:])
+        scatter(0, P, 2 * P)
+        hidden(5, 3)
+        hidden(6, 4)
+        hidden(7, 5)
+        quantize_h(5 * P, 2 * P, h_56[:])
+        quantize_h(7 * P, P, h_last[:])
+        heavy(0, 3 * P, [2 * P], 3)
+        scatter(0, 3 * P, 2 * P)
+        cast_w2(w2_raw[2], h_56[:])
+        heavy(0, 5 * P, [2 * P, P], 6)
+        quantize_w2(2 * P, 2 * P, h_56[:])
+        scatter(0, 5 * P, 3 * P)
         store(0)
-        light(1, 2, 5)
-        light(1, 3, 6)
-        heavy(1, 0, [2 * P], 1)
-        scatter(1, 0, 2 * P)
-        heavy(1, 2 * P, [2 * P], 2)
-        quantize_w2(2 * P, 2 * P, stage_w2(2 * P, 2 * P))
-        heavy(1, BANK, [BANK], 7)
-        scatter(1, 2 * P, 6 * P)
-        store(1)
-        for t in range(2, N // P):
+        for t in range(1, N // P):
             for quarter in range(4):
-                light(t, quarter, 3 + quarter)
-            heavy(t, 0, [BANK], (0, 2)[t - 2])
-            heavy(t, BANK, [BANK], (1, 7)[t - 2])
+                light(t, quarter, quarter)
+            heavy(t, 0, [BANK], (7, 5, 7)[t - 1])
+            heavy(t, BANK, [BANK], (4, 6, 4)[t - 1])
             scatter(t, 0, S)
             store(t)

@@ -51,18 +51,21 @@ def tile_moe_cas_mlp_relu_kernel(
         slot_plane = held("slot_plane", [P, S], U8)
         h_codes = held("h_codes", [P, S], U32)
         h_plane = held("h_plane", [P, S], U8)
-        zeros = held("zeros", [P, P], F32)
+        zeros = reused.tile([P, P], F32, name="zeros", align_bytes=64, offset=0)
         z_rows = [held("z_rows%d" % t, [P, S], F32) for t in range(N // P)]
         result = [held("result%d" % t, [P, T], F32) for t in range(N // P)]
         banks = [psum.tile([P, BANK], F32, name="bank%d" % b) for b in range(8)]
         WORDS = P * PACK
         h_first = held("h_first", [P, WORDS], BF16)
-        h_12 = reused.tile([P, 2 * WORDS], BF16, name="h_12", align_bytes=64, offset=0)
+        early = held("early", [P, 3 * WORDS], BF16)
+        h_12 = early[:, : 2 * WORDS]
+        w2_bf0 = early[:, 3 * WORDS // 2 : 5 * WORDS // 2]
+        w2_bf1 = early[:, 2 * WORDS :]
         w_rest = reused.tile([P, 2 * (N - P)], U8, name="w_rest", align_bytes=64, offset=0)
-        h_34 = held("h_34", [P, 2 * WORDS], BF16)
-        h_56 = held("h_56", [P, 2 * WORDS], BF16)
+        h_36 = held("h_36", [P, 4 * WORDS], BF16)
+        h_34 = h_36[:, : 2 * WORDS]
+        h_56 = h_36[:, 2 * WORDS :]
         h_last = held("h_last", [P, WORDS], BF16)
-        w2_bf1 = held("w2_bf1", [P, WORDS], BF16)
         staged = [h_first[:], h_12[:, :WORDS], h_12[:, WORDS:], h_34[:, :WORDS], h_34[:, WORDS:],
                   h_56[:, :WORDS], h_56[:, WORDS:], h_last[:]]
 
@@ -105,7 +108,7 @@ def tile_moe_cas_mlp_relu_kernel(
         def cast_w2(raw, w2_bf):
             nc.gpsimd.tensor_scalar(
                 w2_bf.rearrange("p (c j) -> p c j", j=PACK),
-                raw[:].rearrange("p j c -> p c j"),
+                raw.rearrange("p j c -> p c j"),
                 1.0,
                 0.0,
                 MULT,
@@ -200,9 +203,9 @@ def tile_moe_cas_mlp_relu_kernel(
         gather_words(0, 2 * P)
         gather_words(2 * P, 2 * P)
         gather_words(4 * P, 4 * P)
-        cast_w2(w2_raw[0], staged[2])
-        quantize_w2(0, P, staged[2])
-        cast_w2(w2_raw[1], w2_bf1[:])
+        cast_w2(w2_raw[0][:], w2_bf0)
+        quantize_w2(0, P, w2_bf0)
+        cast_w2(w2_raw[1][:], w2_bf1)
         hidden(0, 2)
         quantize_h(0, P, h_first[:])
         hidden(1, 3)
@@ -210,25 +213,26 @@ def tile_moe_cas_mlp_relu_kernel(
         hidden(2, 4, on_vector=True)
         light(0, 3, 2, nc.vector.tensor_copy)
         heavy(0, 0, [P], 0)
-        quantize_h(P, 2 * P, h_12[:])
-        nc.sync.dma_start(w_rest[:].bitcast(I32), w_rows[:, P // 2 :])
+        quantize_h(P, 2 * P, h_12)
         scatter(0, 0, P)
+        nc.sync.dma_start(w_rest[:].bitcast(I32), w_rows[:, P // 2 :])
         hidden(3, 3)
         hidden(4, 4)
         heavy(0, P, [2 * P], 5)
-        quantize_h(3 * P, 2 * P, h_34[:])
-        quantize_w2(P, P, w2_bf1[:])
+        quantize_h(3 * P, 2 * P, h_34)
+        quantize_w2(P, P, w2_bf1)
+        cast_w2(w2_raw[2][:, :, :P], staged[4])
         scatter(0, P, 2 * P)
         hidden(5, 3)
         hidden(6, 4)
         hidden(7, 5)
-        quantize_h(5 * P, 2 * P, h_56[:])
+        quantize_h(5 * P, 2 * P, h_56)
         quantize_h(7 * P, P, h_last[:])
         heavy(0, 3 * P, [2 * P], 3)
         scatter(0, 3 * P, 2 * P)
-        cast_w2(w2_raw[2], h_56[:])
+        cast_w2(w2_raw[2][:, :, P:], staged[5])
         heavy(0, 5 * P, [2 * P, P], 6)
-        quantize_w2(2 * P, 2 * P, h_56[:])
+        quantize_w2(2 * P, 2 * P, h_36[:, WORDS : 3 * WORDS])
         scatter(0, 5 * P, 3 * P)
         store(0)
         for t in range(1, N // P):

@@ -189,7 +189,23 @@ def tile_moe_cas_mlp_relu_kernel(
         def store(t):
             nc.sync.dma_start(out[t * P : (t + 1) * P, :], result[t][:])
 
-        nc.vector.tensor_copy(slot_plane[:], x_plane[:].indirect(offsets[:]))
+        ones = held("ones", [P, BANK * PACK], BF16)
+        ones_codes = held("ones_codes", [P, BANK], U32)
+        ones_plane = held("ones_plane", [P, BANK], U8)
+        nc.vector.memset(ones[:].bitcast(I32), 0x3F803F80)
+        nc.vector.quantize_mx(out=ones_codes[:].bitcast(FP8X4), scales=ones_plane[:], in_=ones[:])
+        nc.vector.tensor_copy(slot_plane[:, : 2 * P], x_plane[:].indirect(listed(0, 2 * P)))
+        for warm in range(3):
+            nc.tensor.matmul_mx(
+                out=banks[7][:],
+                lhsT=ones_codes[:, :P].bitcast(FP8X4),
+                lhsT_scale=slot_plane[:, :P],
+                rhs=ones_codes[:].bitcast(FP8X4),
+                rhs_scale=ones_plane[:],
+                start=True,
+                stop=True,
+            )
+        nc.vector.tensor_copy(slot_plane[:, 2 * P :], x_plane[:].indirect(listed(2 * P, S - 2 * P)))
         grouped = w1_bf[:].rearrange("p (t m j) -> p m j t", t=PACK, j=PACK)
         for u in range(2):
             nc.scalar.activation(
@@ -200,45 +216,47 @@ def tile_moe_cas_mlp_relu_kernel(
         nc.vector.quantize_mx(out=w1_codes[:].bitcast(FP8X4), scales=w1_plane[:], in_=w1_bf[:])
         light(0, 0, 0)
         light(0, 1, 1)
+        light(0, 2, 2)
         gather_words(0, 2 * P)
         gather_words(2 * P, 2 * P)
         gather_words(4 * P, 4 * P)
         cast_w2(w2_raw[0][:], w2_bf0)
         quantize_w2(0, P, w2_bf0)
         cast_w2(w2_raw[1][:], w2_bf1)
-        hidden(0, 2)
+        hidden(0, 3)
         quantize_h(0, P, h_first[:])
-        hidden(1, 3)
-        light(0, 2, 1)
-        hidden(2, 4, on_vector=True)
-        light(0, 3, 2, nc.vector.tensor_copy)
+        light(0, 3, 1)
+        hidden(1, 4)
+        hidden(2, 5, on_vector=True)
         heavy(0, 0, [P], 0)
         quantize_h(P, 2 * P, h_12)
         scatter(0, 0, P)
         nc.sync.dma_start(w_rest[:].bitcast(I32), w_rows[:, P // 2 :])
         hidden(3, 3)
-        hidden(4, 4)
-        heavy(0, P, [2 * P], 5)
+        hidden(4, 1)
+        heavy(0, P, [2 * P], 6)
         quantize_h(3 * P, 2 * P, h_34)
         quantize_w2(P, P, w2_bf1)
         cast_w2(w2_raw[2][:, :, :P], staged[4])
         scatter(0, P, 2 * P)
         hidden(5, 3)
-        hidden(6, 4)
-        hidden(7, 5)
+        hidden(6, 1)
+        hidden(7, 6)
         quantize_h(5 * P, 2 * P, h_56)
         quantize_h(7 * P, P, h_last[:])
         heavy(0, 3 * P, [2 * P], 3)
         scatter(0, 3 * P, 2 * P)
         cast_w2(w2_raw[2][:, :, P:], staged[5])
-        heavy(0, 5 * P, [2 * P, P], 6)
+        heavy(0, 5 * P, [2 * P, P], 2)
         quantize_w2(2 * P, 2 * P, h_36[:, WORDS : 3 * WORDS])
         scatter(0, 5 * P, 3 * P)
         store(0)
+        turn = (0, 4, 5, 7, 1, 6, 3, 2)
         for t in range(1, N // P):
+            into = [turn[(6 * (t - 1) + i) % 8] for i in range(6)]
             for quarter in range(4):
-                light(t, quarter, quarter)
-            heavy(t, 0, [BANK], (7, 5, 7)[t - 1])
-            heavy(t, BANK, [BANK], (4, 6, 4)[t - 1])
+                light(t, quarter, into[quarter])
+            heavy(t, 0, [BANK], into[4])
+            heavy(t, BANK, [BANK], into[5])
             scatter(t, 0, S)
             store(t)

@@ -57,10 +57,9 @@ def tile_moe_cas_mlp_relu_kernel(
         banks = [psum.tile([P, BANK], F32, name="bank%d" % b) for b in range(8)]
         WORDS = P * PACK
         h_first = held("h_first", [P, WORDS], BF16)
-        early = held("early", [P, 3 * WORDS], BF16)
-        h_12 = early[:, : 2 * WORDS]
-        w2_bf0 = early[:, 3 * WORDS // 2 : 5 * WORDS // 2]
-        w2_bf1 = early[:, 2 * WORDS :]
+        early = held("early", [P, 2 * WORDS], BF16)
+        h_12 = early[:]
+        w2_bf0 = early[:, WORDS:]
         w_rest = reused.tile([P, 2 * (N - P)], U8, name="w_rest", align_bytes=64, offset=0)
         h_36 = held("h_36", [P, 4 * WORDS], BF16)
         h_34 = h_36[:, : 2 * WORDS]
@@ -222,12 +221,15 @@ def tile_moe_cas_mlp_relu_kernel(
         gather_words(4 * P, 4 * P)
         cast_w2(w2_raw[0][:], w2_bf0)
         quantize_w2(0, P, w2_bf0)
-        cast_w2(w2_raw[1][:], w2_bf1)
         hidden(0, 3)
         quantize_h(0, P, h_first[:])
         light(0, 3, 1)
         hidden(1, 4)
         hidden(2, 5, on_vector=True)
+        nc.vector.tensor_copy(
+            h_first[:].rearrange("p (c i j) -> p c j i", i=4, j=PACK),
+            w2_raw[1][:].rearrange("p j (c i) -> p c j i", i=4),
+        )
         heavy(0, 0, [P], 0)
         quantize_h(P, 2 * P, h_12)
         scatter(0, 0, P)
@@ -236,7 +238,7 @@ def tile_moe_cas_mlp_relu_kernel(
         hidden(4, 1)
         heavy(0, P, [2 * P], 6)
         quantize_h(3 * P, 2 * P, h_34)
-        quantize_w2(P, P, w2_bf1)
+        quantize_w2(P, P, h_first[:])
         cast_w2(w2_raw[2][:, :, :P], staged[4])
         scatter(0, P, 2 * P)
         hidden(5, 3)

@@ -51,15 +51,15 @@ def tile_moe_cas_mlp_relu_kernel(
         slot_plane = held("slot_plane", [P, S], U8)
         h_codes = held("h_codes", [P, S], U32)
         h_plane = held("h_plane", [P, S], U8)
-        zeros = reused.tile([P, P], F32, name="zeros", align_bytes=64, offset=0)
+        zeros = held("zeros", [P, P], F32)
         z_rows = [held("z_rows%d" % t, [P, S], F32) for t in range(N // P)]
         result = [held("result%d" % t, [P, T], F32) for t in range(N // P)]
         banks = [psum.tile([P, BANK], F32, name="bank%d" % b) for b in range(8)]
         WORDS = P * PACK
         h_first = held("h_first", [P, WORDS], BF16)
-        early = held("early", [P, 2 * WORDS], BF16)
+        early = reused.tile([P, 2 * WORDS], BF16, name="early", align_bytes=64, offset=0)
         h_12 = early[:]
-        w2_bf0 = early[:, WORDS:]
+        w2_bf0 = held("w2_bf0", [P, WORDS], BF16)[:]
         w_rest = reused.tile([P, 2 * (N - P)], U8, name="w_rest", align_bytes=64, offset=0)
         h_36 = held("h_36", [P, 4 * WORDS], BF16)
         h_34 = h_36[:, : 2 * WORDS]
@@ -223,17 +223,17 @@ def tile_moe_cas_mlp_relu_kernel(
         quantize_w2(0, P, w2_bf0)
         hidden(0, 3)
         quantize_h(0, P, h_first[:])
-        light(0, 3, 1)
         hidden(1, 4)
-        hidden(2, 5, on_vector=True)
+        light(0, 3, 1)
+        hidden(2, 2, on_vector=True)
         nc.vector.tensor_copy(
             h_first[:].rearrange("p (c i j) -> p c j i", i=4, j=PACK),
             w2_raw[1][:].rearrange("p j (c i) -> p c j i", i=4),
         )
         heavy(0, 0, [P], 0)
         quantize_h(P, 2 * P, h_12)
-        scatter(0, 0, P)
         nc.sync.dma_start(w_rest[:].bitcast(I32), w_rows[:, P // 2 :])
+        scatter(0, 0, P)
         hidden(3, 3)
         hidden(4, 1)
         heavy(0, P, [2 * P], 6)
@@ -249,11 +249,11 @@ def tile_moe_cas_mlp_relu_kernel(
         heavy(0, 3 * P, [2 * P], 3)
         scatter(0, 3 * P, 2 * P)
         cast_w2(w2_raw[2][:, :, P:], staged[5])
-        heavy(0, 5 * P, [2 * P, P], 2)
+        heavy(0, 5 * P, [2 * P, P], 5)
         quantize_w2(2 * P, 2 * P, h_36[:, WORDS : 3 * WORDS])
         scatter(0, 5 * P, 3 * P)
         store(0)
-        turn = (0, 4, 5, 7, 1, 6, 3, 2)
+        turn = (0, 4, 2, 7, 1, 6, 3, 5)
         for t in range(1, N // P):
             into = [turn[(6 * (t - 1) + i) % 8] for i in range(6)]
             for quarter in range(4):

@@ -188,23 +188,7 @@ def tile_moe_cas_mlp_relu_kernel(
         def store(t):
             nc.sync.dma_start(out[t * P : (t + 1) * P, :], result[t][:])
 
-        ones = held("ones", [P, BANK * PACK], BF16)
-        ones_codes = held("ones_codes", [P, BANK], U32)
-        ones_plane = held("ones_plane", [P, BANK], U8)
-        nc.vector.memset(ones[:].bitcast(I32), 0x3F803F80)
-        nc.vector.quantize_mx(out=ones_codes[:].bitcast(FP8X4), scales=ones_plane[:], in_=ones[:])
-        nc.vector.tensor_copy(slot_plane[:, : 2 * P], x_plane[:].indirect(listed(0, 2 * P)))
-        for warm in range(3):
-            nc.tensor.matmul_mx(
-                out=banks[7][:],
-                lhsT=ones_codes[:, :P].bitcast(FP8X4),
-                lhsT_scale=slot_plane[:, :P],
-                rhs=ones_codes[:].bitcast(FP8X4),
-                rhs_scale=ones_plane[:],
-                start=True,
-                stop=True,
-            )
-        nc.vector.tensor_copy(slot_plane[:, 2 * P :], x_plane[:].indirect(listed(2 * P, S - 2 * P)))
+        nc.vector.tensor_copy(slot_plane[:], x_plane[:].indirect(offsets[:]))
         grouped = w1_bf[:].rearrange("p (t m j) -> p m j t", t=PACK, j=PACK)
         for u in range(2):
             nc.scalar.activation(

@@ -60,6 +60,7 @@ def tile_moe_cas_mlp_relu_kernel(
         early = reused.tile([P, 2 * WORDS], BF16, name="early", align_bytes=64, offset=0)
         h_12 = early[:]
         w2_bf0 = held("w2_bf0", [P, WORDS], BF16)[:]
+        w2_bf1 = held("w2_bf1", [P, WORDS], BF16)[:]
         w_rest = reused.tile([P, 2 * (N - P)], U8, name="w_rest", align_bytes=64, offset=0)
         h_36 = held("h_36", [P, 4 * WORDS], BF16)
         h_34 = h_36[:, : 2 * WORDS]
@@ -120,12 +121,12 @@ def tile_moe_cas_mlp_relu_kernel(
                 out=w2_codes[:, cols].bitcast(FP8X4), scales=w2_plane[:, cols], in_=w2_bf
             )
 
-        def light(t, quarter, bank, copy=nc.scalar.copy):
-            tokens = slice(quarter * BANK, (quarter + 1) * BANK)
-            y_acc = banks[bank]
+        def light(t, first, count, bank, copy=nc.scalar.copy):
+            tokens = slice(first, first + count)
+            y_acc = banks[bank][:, :count]
             w_cols = w_head[:] if t == 0 else w_rest[:, 2 * (t - 1) * P : 2 * t * P]
             nc.tensor.matmul_mx(
-                out=y_acc[:],
+                out=y_acc,
                 lhsT=w_cols.bitcast(FP4X4),
                 lhsT_scale=w_plane[:, t * P : (t + 1) * P],
                 rhs=x_codes[:, tokens].bitcast(FP8X4),
@@ -133,7 +134,7 @@ def tile_moe_cas_mlp_relu_kernel(
                 start=True,
                 stop=True,
             )
-            copy(result[t][:, tokens], y_acc[:])
+            copy(result[t][:, tokens], y_acc)
 
         def hidden(c, bank, on_vector=False):
             h_acc = banks[bank]
@@ -197,36 +198,32 @@ def tile_moe_cas_mlp_relu_kernel(
                 COPY,
             )
         nc.vector.quantize_mx(out=w1_codes[:].bitcast(FP8X4), scales=w1_plane[:], in_=w1_bf[:])
-        light(0, 0, 0)
-        light(0, 1, 1)
-        light(0, 2, 2)
+        for piece, bank in enumerate((6, 0, 5, 1, 7, 2)):
+            light(0, piece * 2 * P, 2 * P, bank)
         gather_words(0, 2 * P)
         gather_words(2 * P, 2 * P)
         gather_words(4 * P, 4 * P)
         cast_w2(w2_raw[0][:], w2_bf0)
+        cast_w2(w2_raw[1][:], w2_bf1)
         quantize_w2(0, P, w2_bf0)
         hidden(0, 3)
         quantize_h(0, P, h_first[:])
         hidden(1, 4)
-        light(0, 3, 1)
-        hidden(2, 2, on_vector=True)
-        nc.vector.tensor_copy(
-            h_first[:].rearrange("p (c i j) -> p c j i", i=4, j=PACK),
-            w2_raw[1][:].rearrange("p j (c i) -> p c j i", i=4),
-        )
+        light(0, 3 * BANK, BANK, 2)
+        hidden(2, 7, on_vector=True)
         heavy(0, 0, [P], 0)
         quantize_h(P, 2 * P, h_12)
         nc.sync.dma_start(w_rest[:].bitcast(I32), w_rows[:, P // 2 :])
         scatter(0, 0, P)
         hidden(3, 3)
-        hidden(4, 1)
+        hidden(4, 2)
         heavy(0, P, [2 * P], 6)
         quantize_h(3 * P, 2 * P, h_34)
-        quantize_w2(P, P, h_first[:])
+        quantize_w2(P, P, w2_bf1)
         cast_w2(w2_raw[2][:, :, :P], staged[4])
         scatter(0, P, 2 * P)
         hidden(5, 3)
-        hidden(6, 1)
+        hidden(6, 2)
         hidden(7, 6)
         quantize_h(5 * P, 2 * P, h_56)
         quantize_h(7 * P, P, h_last[:])
@@ -237,11 +234,11 @@ def tile_moe_cas_mlp_relu_kernel(
         quantize_w2(2 * P, 2 * P, h_36[:, WORDS : 3 * WORDS])
         scatter(0, 5 * P, 3 * P)
         store(0)
-        turn = (0, 4, 2, 7, 1, 6, 3, 5)
+        turn = (0, 4, 7, 1, 2, 6, 3, 5)
         for t in range(1, N // P):
             into = [turn[(6 * (t - 1) + i) % 8] for i in range(6)]
             for quarter in range(4):
-                light(t, quarter, into[quarter])
+                light(t, quarter * BANK, BANK, into[quarter])
             heavy(t, 0, [BANK], into[4])
             heavy(t, BANK, [BANK], into[5])
             scatter(t, 0, S)

@@ -234,12 +234,23 @@ def tile_moe_cas_mlp_relu_kernel(
         quantize_w2(2 * P, 2 * P, h_36[:, WORDS : 3 * WORDS])
         scatter(0, 5 * P, 3 * P)
         store(0)
-        turn = (0, 4, 7, 1, 2, 6, 3, 5)
-        for t in range(1, N // P):
-            into = [turn[(6 * (t - 1) + i) % 8] for i in range(6)]
-            for quarter in range(4):
-                light(t, quarter * BANK, BANK, into[quarter])
-            heavy(t, 0, [BANK], into[4])
-            heavy(t, BANK, [BANK], into[5])
-            scatter(t, 0, S)
-            store(t)
+        for quarter, bank in enumerate((0, 4, 7, 1)):
+            light(1, quarter * BANK, BANK, bank)
+        heavy(1, 0, [BANK], 2)
+        scatter(1, 0, BANK)
+        for quarter, bank in enumerate((6, 3, 5, 0)):
+            light(2, quarter * BANK, BANK, bank)
+        heavy(2, 0, [BANK], 4)
+        scatter(2, 0, BANK)
+        heavy(1, BANK, [BANK], 0)
+        scatter(1, BANK, BANK)
+        store(1)
+        heavy(2, BANK, [BANK], 4)
+        scatter(2, BANK, BANK)
+        store(2)
+        for quarter, bank in enumerate((0, 4, 0, 4)):
+            light(3, quarter * BANK, BANK, bank)
+        heavy(3, 0, [BANK], 7)
+        heavy(3, BANK, [BANK], 1)
+        scatter(3, 0, S)
+        store(3)

@@ -191,12 +191,10 @@ def tile_moe_cas_mlp_relu_kernel(
 
         nc.vector.tensor_copy(slot_plane[:], x_plane[:].indirect(offsets[:]))
         grouped = w1_bf[:].rearrange("p (t m j) -> p m j t", t=PACK, j=PACK)
-        for u in range(2):
-            nc.scalar.activation(
-                grouped[:, u * P // 2 : (u + 1) * P // 2],
-                w1_raw[u][:].rearrange("p j (m t) -> p m j t", t=PACK),
-                COPY,
-            )
+        halves = [raw[:].rearrange("p j (m t) -> p m j t", t=PACK) for raw in w1_raw]
+        nc.scalar.activation(grouped[:, : P // 2], halves[0], COPY)
+        nc.scalar.activation(grouped[:, P // 2 :, :, :3], halves[1][:, :, :, :3], COPY)
+        nc.gpsimd.tensor_scalar(grouped[:, P // 2 :, :, 3], halves[1][:, :, :, 3], 1.0, 0.0, MULT, ADD)
         nc.vector.quantize_mx(out=w1_codes[:].bitcast(FP8X4), scales=w1_plane[:], in_=w1_bf[:])
         for piece, bank in enumerate((6, 0, 5, 1, 7, 2)):
             light(0, piece * 2 * P, 2 * P, bank)

@@ -161,7 +161,7 @@ def tile_moe_cas_mlp_relu_kernel(
                 out=h_codes[:, slots].bitcast(FP8X4), scales=h_plane[:, slots], in_=h_bf
             )
 
-        def heavy(t, first, widths, bank):
+        def heavy(t, first, widths, bank, copy=nc.scalar.copy):
             z_acc = banks[bank]
             at = 0
             for count in widths:
@@ -176,7 +176,7 @@ def tile_moe_cas_mlp_relu_kernel(
                     stop=True,
                 )
                 at += count
-            nc.scalar.copy(z_rows[t][:, first : first + at], z_acc[:, :at])
+            copy(z_rows[t][:, first : first + at], z_acc[:, :at])
 
         def scatter(t, first, count):
             window = result[t][:].indirect(listed(first, count))
@@ -186,8 +186,12 @@ def tile_moe_cas_mlp_relu_kernel(
             else:
                 nc.vector.tensor_copy(window, values)
 
-        def store(t):
-            nc.sync.dma_start(out[t * P : (t + 1) * P, :], result[t][:])
+        def scatter_on_scalar(t, first, count):
+            window = result[t][:].indirect(listed(first, count))
+            nc.scalar.activation(window, z_rows[t][:, first : first + count], COPY)
+
+        def store(t, queue=nc.sync):
+            queue.dma_start(out[t * P : (t + 1) * P, :], result[t][:])
 
         nc.vector.tensor_copy(slot_plane[:], x_plane[:].indirect(offsets[:]))
         grouped = w1_bf[:].rearrange("p (t m j) -> p m j t", t=PACK, j=PACK)
@@ -236,19 +240,19 @@ def tile_moe_cas_mlp_relu_kernel(
             light(1, quarter * BANK, BANK, bank)
         heavy(1, 0, [BANK], 2)
         scatter(1, 0, BANK)
-        for quarter, bank in enumerate((6, 3, 5, 0)):
-            light(2, quarter * BANK, BANK, bank)
-        heavy(2, 0, [BANK], 4)
-        scatter(2, 0, BANK)
-        heavy(1, BANK, [BANK], 0)
+        heavy(1, BANK, [BANK], 6)
+        heavy(3, 0, [BANK], 3, nc.vector.tensor_copy)
+        heavy(3, BANK, [BANK], 5, nc.vector.tensor_copy)
         scatter(1, BANK, BANK)
         store(1)
-        heavy(2, BANK, [BANK], 4)
-        scatter(2, BANK, BANK)
-        store(2)
-        for quarter, bank in enumerate((0, 4, 0, 4)):
+        for quarter, bank in enumerate((0, 4, 7, 1)):
+            light(2, quarter * BANK, BANK, bank)
+        heavy(2, 0, [BANK], 2)
+        heavy(2, BANK, [BANK], 6)
+        for quarter, bank in enumerate((0, 4, 7, 1)):
             light(3, quarter * BANK, BANK, bank)
-        heavy(3, 0, [BANK], 7)
-        heavy(3, BANK, [BANK], 1)
+        for first, count in ((0, 3 * P), (3 * P, 3 * P), (6 * P, 2 * P)):
+            scatter_on_scalar(2, first, count)
+        store(2, nc.scalar)
         scatter(3, 0, S)
         store(3)

@@ -242,17 +242,19 @@ def tile_moe_cas_mlp_relu_kernel(
         scatter(1, 0, BANK)
         heavy(1, BANK, [BANK], 6)
         heavy(3, 0, [BANK], 3, nc.vector.tensor_copy)
-        heavy(3, BANK, [BANK], 5, nc.vector.tensor_copy)
+        heavy(3, BANK, [2 * P], 5, nc.vector.tensor_copy)
         scatter(1, BANK, BANK)
         store(1)
         for quarter, bank in enumerate((0, 4, 7, 1)):
             light(2, quarter * BANK, BANK, bank)
         heavy(2, 0, [BANK], 2)
         heavy(2, BANK, [BANK], 6)
+        scatter_on_scalar(2, 0, 2 * P)
         for quarter, bank in enumerate((0, 4, 7, 1)):
             light(3, quarter * BANK, BANK, bank)
-        for first, count in ((0, 3 * P), (3 * P, 3 * P), (6 * P, 2 * P)):
-            scatter_on_scalar(2, first, count)
+        heavy(3, 6 * P, [2 * P], 2)
+        scatter_on_scalar(2, 2 * P, 3 * P)
+        scatter_on_scalar(2, 5 * P, 3 * P)
         store(2, nc.scalar)
         scatter(3, 0, S)
         store(3)

@@ -30,7 +30,6 @@ def tile_moe_cas_mlp_relu_kernel(
     nc = tc.nc
     with ExitStack() as ctx:
         keep = ctx.enter_context(tc.tile_pool(name="keep", bufs=1))
-        reused = ctx.enter_context(tc.tile_pool(name="reused", bufs=1))
         psum = ctx.enter_context(tc.psum_pool(name="psum", bufs=1))
 
         def held(name, shape, dtype):
@@ -57,11 +56,10 @@ def tile_moe_cas_mlp_relu_kernel(
         banks = [psum.tile([P, BANK], F32, name="bank%d" % b) for b in range(8)]
         WORDS = P * PACK
         h_first = held("h_first", [P, WORDS], BF16)
-        early = reused.tile([P, 2 * WORDS], BF16, name="early", align_bytes=64, offset=0)
-        h_12 = early[:]
+        h_12 = held("h_12", [P, 2 * WORDS], BF16)[:]
         w2_bf0 = held("w2_bf0", [P, WORDS], BF16)[:]
         w2_bf1 = held("w2_bf1", [P, WORDS], BF16)[:]
-        w_rest = reused.tile([P, 2 * (N - P)], U8, name="w_rest", align_bytes=64, offset=0)
+        w_rest = held("w_rest", [P, 2 * (N - P)], U8)
         h_36 = held("h_36", [P, 4 * WORDS], BF16)
         h_34 = h_36[:, : 2 * WORDS]
         h_56 = h_36[:, 2 * WORDS :]
@@ -93,6 +91,7 @@ def tile_moe_cas_mlp_relu_kernel(
         nc.sync.dma_start(w2_raw[0][:], w2_rows[:, :, :P])
         nc.sync.dma_start(w2_raw[1][:], w2_rows[:, :, P : 2 * P])
         nc.sync.dma_start(w2_raw[2][:], w2_rows[:, :, 2 * P :])
+        nc.sync.dma_start(w_rest[:].bitcast(I32), w_rows[:, P // 2 :])
 
         slot_codes = {}
 
@@ -215,9 +214,8 @@ def tile_moe_cas_mlp_relu_kernel(
         hidden(2, 7, on_vector=True)
         heavy(0, 0, [P], 0)
         quantize_h(P, 2 * P, h_12)
-        nc.sync.dma_start(w_rest[:].bitcast(I32), w_rows[:, P // 2 :])
         scatter(0, 0, P)
-        hidden(3, 3)
+        hidden(3, 3, on_vector=True)
         hidden(4, 2)
         heavy(0, P, [2 * P], 6)
         quantize_h(3 * P, 2 * P, h_34)
@@ -230,29 +228,30 @@ def tile_moe_cas_mlp_relu_kernel(
         quantize_h(5 * P, 2 * P, h_56)
         quantize_h(7 * P, P, h_last[:])
         heavy(0, 3 * P, [2 * P], 3)
+        light(1, 0, BANK, 2)
+        light(1, BANK, BANK, 6)
         scatter(0, 3 * P, 2 * P)
         cast_w2(w2_raw[2][:, :, P:], staged[5])
         heavy(0, 5 * P, [2 * P, P], 5)
         quantize_w2(2 * P, 2 * P, h_36[:, WORDS : 3 * WORDS])
         scatter(0, 5 * P, 3 * P)
         store(0)
-        for quarter, bank in enumerate((0, 4, 7, 1)):
-            light(1, quarter * BANK, BANK, bank)
-        heavy(1, 0, [BANK], 2)
+        light(1, 2 * BANK, BANK, 3)
+        light(1, 3 * BANK, BANK, 2)
+        heavy(1, 0, [BANK], 5)
         scatter(1, 0, BANK)
-        heavy(1, BANK, [BANK], 6)
-        heavy(3, 0, [BANK], 3, nc.vector.tensor_copy)
-        heavy(3, BANK, [2 * P], 5, nc.vector.tensor_copy)
+        heavy(1, BANK, [BANK], 0)
+        heavy(3, 0, [BANK], 5, nc.vector.tensor_copy)
+        heavy(3, BANK, [BANK], 2, nc.vector.tensor_copy)
         scatter(1, BANK, BANK)
         store(1)
-        for quarter, bank in enumerate((0, 4, 7, 1)):
+        for quarter, bank in enumerate((6, 3, 0, 6)):
             light(2, quarter * BANK, BANK, bank)
-        heavy(2, 0, [BANK], 2)
-        heavy(2, BANK, [BANK], 6)
+        heavy(2, 0, [BANK], 3)
+        heavy(2, BANK, [BANK], 0)
         scatter_on_scalar(2, 0, 2 * P)
-        for quarter, bank in enumerate((0, 4, 7, 1)):
+        for quarter, bank in enumerate((6, 3, 0, 6)):
             light(3, quarter * BANK, BANK, bank)
-        heavy(3, 6 * P, [2 * P], 2)
         scatter_on_scalar(2, 2 * P, 3 * P)
         scatter_on_scalar(2, 5 * P, 3 * P)
         store(2, nc.scalar)

@@ -254,6 +254,6 @@ def tile_moe_cas_mlp_relu_kernel(
             light(3, quarter * BANK, BANK, bank)
         scatter_on_scalar(2, 2 * P, 3 * P)
         scatter_on_scalar(2, 5 * P, 3 * P)
-        store(2, nc.scalar)
+        store(2)
         scatter(3, 0, S)
-        store(3)
+        store(3, nc.scalar)

from contextlib import ExitStack

import concourse.mybir as mybir

K, T, S, H, N = 512, 2048, 1024, 512, 512
FLOPS = 2 * K * N * T + 2 * K * H * S + 2 * H * N * S

F32 = mybir.dt.float32
BF16 = mybir.dt.bfloat16
I32 = mybir.dt.int32
U32 = mybir.dt.uint32
U16 = mybir.dt.uint16
U8 = mybir.dt.uint8
FP8X4 = mybir.dt.float8_e4m3fn_x4
FP4X4 = mybir.dt.float4_e2m1fn_x4
COPY = mybir.ActivationFunctionType.Copy
RELU = mybir.ActivationFunctionType.Relu
ADD = mybir.AluOpType.add
MULT = mybir.AluOpType.mult

P = 128
PACK = 4
BANK = 512
STRIPE = 16


def tile_moe_cas_mlp_relu_kernel(
    tc, x_words, x_scales, w_words, w_scales, w1, w2, offs, out
):
    nc = tc.nc
    with ExitStack() as ctx:
        keep = ctx.enter_context(tc.tile_pool(name="keep", bufs=1))
        psum = ctx.enter_context(tc.psum_pool(name="psum", bufs=1))

        def held(name, shape, dtype):
            return keep.tile(shape, dtype, name=name, align_bytes=64)

        offsets = keep.tile([P, S // STRIPE], U16)
        x_codes = held("x_codes", [P, T], I32)
        x_plane = held("x_plane", [P, T], U8)
        w_head = held("w_head", [P, 2 * P], U8)
        w_plane = held("w_plane", [P, N], U8)
        w1_raw = [held("w1_raw%d" % u, [P, PACK, H // 2], F32) for u in range(2)]
        w2_raw = [held("w2_raw%d" % u, [P, PACK, c], F32) for u, c in enumerate((P, P, 2 * P))]
        w1_bf = held("w1_bf", [P, H * PACK], BF16)
        w1_codes = held("w1_codes", [P, H], U32)
        w1_plane = held("w1_plane", [P, H], U8)
        w2_codes = held("w2_codes", [P, N], U32)
        w2_plane = held("w2_plane", [P, N], U8)
        slot_plane = held("slot_plane", [P, S], U8)
        h_codes = held("h_codes", [P, S], U32)
        h_plane = held("h_plane", [P, S], U8)
        zeros = held("zeros", [P, P], F32)
        z_rows = [held("z_rows%d" % t, [P, S], F32) for t in range(N // P)]
        result = [held("result%d" % t, [P, T], F32) for t in range(N // P)]
        banks = [psum.tile([P, BANK], F32, name="bank%d" % b) for b in range(8)]
        WORDS = P * PACK
        h_first = held("h_first", [P, WORDS], BF16)
        h_12 = held("h_12", [P, 2 * WORDS], BF16)[:]
        w2_bf0 = held("w2_bf0", [P, WORDS], BF16)[:]
        w2_bf1 = held("w2_bf1", [P, WORDS], BF16)[:]
        w_rest = held("w_rest", [P, 2 * (N - P)], U8)
        h_36 = held("h_36", [P, 4 * WORDS], BF16)
        h_34 = h_36[:, : 2 * WORDS]
        h_56 = h_36[:, 2 * WORDS :]
        h_last = held("h_last", [P, WORDS], BF16)
        staged = [h_first[:], h_12[:, :WORDS], h_12[:, WORDS:], h_34[:, :WORDS], h_34[:, WORDS:],
                  h_56[:, :WORDS], h_56[:, WORDS:], h_last[:]]

        nc.vector.memset(x_plane[:].bitcast(I32), 0)
        nc.gpsimd.memset(w_plane[:].bitcast(I32), 0)
        nc.gpsimd.memset(zeros[:], 0.0)
        w1_rows = w1.rearrange("(p j) c -> p j c", j=PACK)
        w2_rows = w2.rearrange("(p j) c -> p j c", j=PACK)
        x_rows = x_words[0].rearrange("p t d -> p (t d)").bitcast(I32)
        nc.sync.dma_start(w1_raw[0][:], w1_rows[:, :, : H // 2])
        nc.sync.dma_start(offsets[:], offs)
        for r in range(PACK):
            nc.sync.dma_start(
                x_plane[r:P:32, :].bitcast(I32), x_scales[0, r:16:PACK, :].bitcast(I32)
            )
        nc.sync.dma_start(w1_raw[1][:], w1_rows[:, :, H // 2 :])
        nc.sync.dma_start(x_codes[:, : T // 2], x_rows[:, : T // 2])
        w_rows = w_words[0].bitcast(I32)
        nc.sync.dma_start(w_head[:].bitcast(I32), w_rows[:, : P // 2])
        for r in range(PACK):
            nc.sync.dma_start(
                w_plane[r:P:32, :].bitcast(I32), w_scales[0, r:16:PACK, :].bitcast(I32)
            )
        nc.sync.dma_start(x_codes[:, T // 2 :], x_rows[:, T // 2 :])
        nc.sync.dma_start(w2_raw[0][:], w2_rows[:, :, :P])
        nc.sync.dma_start(w2_raw[1][:], w2_rows[:, :, P : 2 * P])
        nc.sync.dma_start(w2_raw[2][:], w2_rows[:, :, 2 * P :])
        nc.sync.dma_start(w_rest[:].bitcast(I32), w_rows[:, P // 2 :])

        slot_codes = {}

        def listed(first, count):
            return offsets[:, first // STRIPE : (first + count) // STRIPE]

        def gather_words(first, count):
            codes = held("slot_codes%d" % first, [P, count], U32)
            nc.vector.tensor_copy(codes[:], x_codes[:].bitcast(U32).indirect(listed(first, count)))
            for c in range(count // P):
                slot_codes[first // P + c] = codes[:, c * P : (c + 1) * P]

        def cast_w2(raw, w2_bf):
            nc.gpsimd.tensor_scalar(
                w2_bf.rearrange("p (c j) -> p c j", j=PACK),
                raw.rearrange("p j c -> p c j"),
                1.0,
                0.0,
                MULT,
                ADD,
            )

        def quantize_w2(first, count, w2_bf):
            cols = slice(first, first + count)
            nc.vector.quantize_mx(
                out=w2_codes[:, cols].bitcast(FP8X4), scales=w2_plane[:, cols], in_=w2_bf
            )

        def light(t, first, count, bank, copy=nc.scalar.copy):
            tokens = slice(first, first + count)
            y_acc = banks[bank][:, :count]
            w_cols = w_head[:] if t == 0 else w_rest[:, 2 * (t - 1) * P : 2 * t * P]
            nc.tensor.matmul_mx(
                out=y_acc,
                lhsT=w_cols.bitcast(FP4X4),
                lhsT_scale=w_plane[:, t * P : (t + 1) * P],
                rhs=x_codes[:, tokens].bitcast(FP8X4),
                rhs_scale=x_plane[:, tokens],
                start=True,
                stop=True,
            )
            copy(result[t][:, tokens], y_acc)

        def hidden(c, bank, on_vector=False):
            h_acc = banks[bank]
            for j in range(PACK):
                nc.tensor.matmul_mx(
                    out=h_acc[:, j * P : (j + 1) * P],
                    lhsT=w1_codes[:, j * P : (j + 1) * P].bitcast(FP8X4),
                    lhsT_scale=w1_plane[:, j * P : (j + 1) * P],
                    rhs=slot_codes[c].bitcast(FP8X4),
                    rhs_scale=slot_plane[:, c * P : (c + 1) * P],
                    start=True,
                    stop=True,
                )
            dst = staged[c].rearrange("p (s j) -> p s j", j=PACK)
            src = h_acc[:].rearrange("p (j s) -> p s j", j=PACK)
            if on_vector:
                nc.vector.tensor_scalar_max(dst, src, 0.0)
            else:
                nc.scalar.activation(dst, src, RELU)

        def quantize_h(first, count, h_bf):
            slots = slice(first, first + count)
            nc.vector.quantize_mx(
                out=h_codes[:, slots].bitcast(FP8X4), scales=h_plane[:, slots], in_=h_bf
            )

        def heavy(t, first, widths, bank, copy=nc.scalar.copy):
            z_acc = banks[bank]
            at = 0
            for count in widths:
                slots = slice(first + at, first + at + count)
                nc.tensor.matmul_mx(
                    out=z_acc[:, at : at + count],
                    lhsT=w2_codes[:, t * P : (t + 1) * P].bitcast(FP8X4),
                    lhsT_scale=w2_plane[:, t * P : (t + 1) * P],
                    rhs=h_codes[:, slots].bitcast(FP8X4),
                    rhs_scale=h_plane[:, slots],
                    start=True,
                    stop=True,
                )
                at += count
            copy(z_rows[t][:, first : first + at], z_acc[:, :at])

        def scatter(t, first, count):
            window = result[t][:].indirect(listed(first, count))
            values = z_rows[t][:, first : first + count]
            if count == P:
                nc.vector.tensor_tensor(window, values, zeros[:], ADD)
            else:
                nc.vector.tensor_copy(window, values)

        def scatter_on_scalar(t, first, count):
            window = result[t][:].indirect(listed(first, count))
            nc.scalar.activation(window, z_rows[t][:, first : first + count], COPY)

        def store(t, queue=nc.sync):
            queue.dma_start(out[t * P : (t + 1) * P, :], result[t][:])

        nc.vector.tensor_copy(slot_plane[:], x_plane[:].indirect(offsets[:]))
        grouped = w1_bf[:].rearrange("p (t m j) -> p m j t", t=PACK, j=PACK)
        halves = [raw[:].rearrange("p j (m t) -> p m j t", t=PACK) for raw in w1_raw]
        nc.scalar.activation(grouped[:, : P // 2], halves[0], COPY)
        nc.scalar.activation(grouped[:, P // 2 :, :, :3], halves[1][:, :, :, :3], COPY)
        nc.gpsimd.tensor_scalar(grouped[:, P // 2 :, :, 3], halves[1][:, :, :, 3], 1.0, 0.0, MULT, ADD)
        nc.vector.quantize_mx(out=w1_codes[:].bitcast(FP8X4), scales=w1_plane[:], in_=w1_bf[:])
        for piece, bank in enumerate((6, 0, 5, 1, 7, 2)):
            light(0, piece * 2 * P, 2 * P, bank)
        gather_words(0, 2 * P)
        gather_words(2 * P, 2 * P)
        gather_words(4 * P, 4 * P)
        cast_w2(w2_raw[0][:], w2_bf0)
        cast_w2(w2_raw[1][:], w2_bf1)
        quantize_w2(0, P, w2_bf0)
        hidden(0, 3)
        quantize_h(0, P, h_first[:])
        hidden(1, 4)
        light(0, 3 * BANK, BANK, 2)
        hidden(2, 7, on_vector=True)
        heavy(0, 0, [P], 0)
        quantize_h(P, 2 * P, h_12)
        scatter(0, 0, P)
        hidden(3, 3, on_vector=True)
        hidden(4, 2)
        heavy(0, P, [2 * P], 6)
        quantize_h(3 * P, 2 * P, h_34)
        quantize_w2(P, P, w2_bf1)
        cast_w2(w2_raw[2][:, :, :P], staged[4])
        scatter(0, P, 2 * P)
        hidden(5, 3)
        hidden(6, 2)
        hidden(7, 6)
        quantize_h(5 * P, 2 * P, h_56)
        quantize_h(7 * P, P, h_last[:])
        heavy(0, 3 * P, [2 * P], 3)
        light(1, 0, BANK, 2)
        light(1, BANK, BANK, 6)
        scatter(0, 3 * P, 2 * P)
        cast_w2(w2_raw[2][:, :, P:], staged[5])
        heavy(0, 5 * P, [2 * P, P], 5)
        quantize_w2(2 * P, 2 * P, h_36[:, WORDS : 3 * WORDS])
        scatter(0, 5 * P, 3 * P)
        store(0)
        light(1, 2 * BANK, BANK, 3)
        light(1, 3 * BANK, BANK, 2)
        heavy(1, 0, [BANK], 5)
        scatter(1, 0, BANK)
        heavy(1, BANK, [BANK], 0)
        heavy(3, 0, [BANK], 5, nc.vector.tensor_copy)
        heavy(3, BANK, [BANK], 2, nc.vector.tensor_copy)
        scatter(1, BANK, BANK)
        store(1)
        for quarter, bank in enumerate((6, 3, 0, 6)):
            light(2, quarter * BANK, BANK, bank)
        heavy(2, 0, [BANK], 3)
        heavy(2, BANK, [BANK], 0)
        scatter_on_scalar(2, 0, 2 * P)
        for quarter, bank in enumerate((6, 3, 0, 6)):
            light(3, quarter * BANK, BANK, bank)
        scatter_on_scalar(2, 2 * P, 3 * P)
        scatter_on_scalar(2, 5 * P, 3 * P)
        store(2)
        scatter(3, 0, S)
        store(3, nc.scalar)
